import numpy as np
import ml_dtypes


def mxq(x, axis, fmt="e4m3"):
    dtype, down = {"e4m3": (ml_dtypes.float8_e4m3fn, 7), "e5m2": (ml_dtypes.float8_e5m2, 14)}[fmt]
    v = np.moveaxis(np.asarray(x, np.float32).astype(ml_dtypes.bfloat16).astype(np.float64), axis, -1)
    blocks = v.reshape(v.shape[:-1] + (-1, 32))
    amax = np.abs(blocks).max(-1, keepdims=True)
    byte = np.maximum(np.where(amax > 0, np.frexp(amax)[1] - 1 + 127, 0) - down, 1)
    scale = np.exp2(byte - 127.0)
    codes = (blocks / scale).astype(np.float32).astype(dtype).astype(np.float64)
    return np.moveaxis((codes * scale).reshape(v.shape), -1, axis)


WIDE = False


def mx_kscale(k):
    if not WIDE:
        return np.ones(k)
    levels = np.array([10, -10, 5, -5, 0])
    if k % 512:
        return np.exp2(np.random.permutation(np.resize(levels, k // 32))).repeat(32)
    a = np.empty((k // 512, 16))
    for p in range(k // 512):
        a[p, :8] = np.random.permutation(np.resize(levels, 8))
        for g in range(8):
            far = levels[np.abs(levels - a[p, g]) >= 10]
            a[p, g + 8] = far[np.random.randint(len(far))]
    return np.exp2(a.ravel()).repeat(32)


BF16 = ml_dtypes.bfloat16


def bf(x):
    return np.asarray(x, np.float32).astype(BF16)


def f64(x):
    return np.asarray(x).astype(np.float64)


U, I, J, B = 1024, 1024, 1024, 1024

SHRINK_SIM = 0.5
SHRINK_DAMP = 0.5


def draw0():
    su, t = mx_kscale(U), mx_kscale(J)
    return {"p": bf(np.random.standard_normal((U, I)) * su[:, None]),
            "v": bf(np.random.standard_normal((U, J)) / su[:, None]),
            "n_p": bf(np.random.uniform(0.5, 1.5, I)),
            "n_v": bf(np.random.uniform(0.5, 1.5, J)),
            "g": bf((1.0 + 0.1 * np.random.standard_normal(J)) * t),
            "h": bf(np.random.standard_normal((B, J)) / np.sqrt(J) / t[None, :])}


def cross_occurrence(p, v):
    users = p.shape[0]
    return (mxq(p, 0, "e4m3").T @ mxq(v, 0, "e4m3")) / np.sqrt(users)


def damped_similarity(c, n_p, n_v, g):
    sim = c / (n_p[:, None] * n_v[None, :] + SHRINK_SIM)
    mag = np.abs(c)
    damp = mag / (mag + SHRINK_DAMP)
    return sim * damp * g[None, :]


def core(p, v, n_p, n_v, g, h):
    c = cross_occurrence(f64(p), f64(v))
    s = damped_similarity(c, f64(n_p), f64(n_v), f64(g))
    return mxq(f64(h), 1, "e4m3") @ mxq(s, 1, "e4m3").T


def e4m3fn_bytes(y):
    return np.clip(np.asarray(y, np.float64), -448.0, 448.0).astype(np.float32).astype(ml_dtypes.float8_e4m3fn).view(np.uint8)


def e4m3fn_values(b):
    return np.asarray(b, np.uint8).view(ml_dtypes.float8_e4m3fn).astype(np.float64)


def setup_inputs():
    d = draw0()
    x0 = np.asarray(d['v']).astype(np.float64)
    s = (np.max(np.abs(x0), axis=(1,), keepdims=True) / 448.0).astype(np.float32)
    out = {}
    for k, v in d.items():
        if k == 'v':
            out['v_bytes'] = e4m3fn_bytes(x0 / s.astype(np.float64))
            out['v_scale'] = s
        else:
            out[k] = v
    return out


def reference(p, v_bytes, v_scale, n_p, n_v, g, h):
    return core(p, e4m3fn_values(v_bytes) * v_scale.astype(np.float64), n_p, n_v, g, h)

@@ -1,0 +1,460 @@
+from contextlib import ExitStack
+
+import concourse.mybir as mybir
+from concourse.masks import make_identity
+
+U = I = J = B = 1024
+FLOPS = 2 * U * I * J + 2 * B * I * J
+
+F32 = mybir.dt.float32
+BF16 = mybir.dt.bfloat16
+U32 = mybir.dt.uint32
+U8 = mybir.dt.uint8
+FP8 = mybir.dt.float8_e4m3fn
+FP8X4 = mybir.dt.float8_e4m3fn_x4
+ACT = mybir.ActivationFunctionType
+ALU = mybir.AluOpType
+
+P = 128
+T = 4
+KP = P * T
+ROOT_U = 32.0
+SHRINK_SIM = 0.5
+SHRINK_DAMP = 0.5
+DAMP = ROOT_U * SHRINK_DAMP
+C_FLOOR = 2.0 ** -60
+G_FLOOR = 2.0 ** -50
+
+BANKS = [(c, half) for half in range(2) for c in range(4)] + [(c, half) for c in range(4, 8) for half in range(2)]
+
+
+def tile_crossoccurrencedampedscores_kernel(tc, p, v_bytes, v_scale, n_p, n_v, g, h, out):
+    nc = tc.nc
+    with ExitStack() as ctx:
+        keep = ctx.enter_context(tc.tile_pool(name="keep", bufs=1))
+        work = ctx.enter_context(tc.tile_pool(name="work", bufs=3))
+        psum = ctx.enter_context(tc.psum_pool(name="psum", bufs=1))
+        ctx.enter_context(tc.manual_schedule())
+
+        def kept(shape, dtype, name):
+            return keep.tile(shape, dtype, name=name, align_bytes=64)
+
+        def mx_tiles(width, name):
+            return kept([P, width], U32, name + "_codes"), kept([P, width], U8, name + "_scales")
+
+        def side_bank(shape, dtype):
+            return psum.tile(shape, dtype, name="side", tag="side", bufs=3)
+
+        vs = kept([P, 2, T], F32, "vs")
+        g_sb = kept([P, 2, T], BF16, "g_sb")
+        nv_sb = kept([P, 2, T], BF16, "nv_sb")
+        d_rhs = kept([P, I], BF16, "d_rhs")
+        floor_col = kept([P, 1], F32, "floor_col")
+        nc.vector.memset(floor_col[:], C_FLOOR)
+        nc.vector.memset(d_rhs[:], 1.0)
+        nc.scalar.dma_start(out=vs[:], in_=v_scale.rearrange("(a p t) o -> p a (t o)", p=P, t=T))
+
+        v_rows = v_bytes.rearrange("(a p t) j -> a p t j", p=P, t=T)
+        p_rows = p.rearrange("(a p t) i -> a p t i", p=P, t=T)
+        h_rows = h.rearrange("(q r p) j -> q p r j", p=P, r=2)
+        v_raw, p_raw, h_raw = {}, {}, {}
+
+        def load_v(a, half):
+            v_raw[a, half] = kept([P, T, KP], U8, "v_raw_%d_%d" % (a, half))
+            nc.sync.dma_start(out=v_raw[a, half][:], in_=v_rows[a][:, :, half * KP:(half + 1) * KP])
+
+        def load_p(a, quarter):
+            p_raw[a, quarter] = kept([P, T, 256], BF16, "p_raw_%d_%d" % (a, quarter))
+            nc.sync.dma_start(out=p_raw[a, quarter][:], in_=p_rows[a][:, :, quarter * 256:(quarter + 1) * 256])
+
+        def load_h(pair):
+            h_raw[pair] = kept([P, 2, J], BF16, "h_raw_%d" % pair)
+            nc.sync.dma_start(out=h_raw[pair][:], in_=h_rows[pair])
+
+        load_v(0, 0)
+        nc.sync.dma_start(out=g_sb[:], in_=g.rearrange("(a p t) -> p a t", p=P, t=T))
+        nc.sync.dma_start(out=nv_sb[:], in_=n_v.rearrange("(a p t) -> p a t", p=P, t=T))
+        load_v(1, 0)
+        for a in range(2):
+            load_p(a, 0)
+        nc.sync.dma_start(out=d_rhs[0:4, :], in_=n_p.partition_broadcast(4))
+        load_v(0, 1)
+        for a in range(2):
+            load_p(a, 1)
+        load_v(1, 1)
+        load_h(0)
+        for a in range(2):
+            load_p(a, 2)
+        load_h(1)
+        for a in range(2):
+            load_p(a, 3)
+        load_h(2)
+        load_h(3)
+
+        ident_bf = kept([P, P], BF16, "ident_bf")
+        ident_f = kept([P, P], F32, "ident_f")
+        table_probe = kept([P, 1], F32, "table_probe")
+        pieces = kept([P, 8, P], BF16, "pieces")
+        nc.vector.memset(pieces[:], 0.0)
+        nc.scalar.activation(out=table_probe[:], in_=floor_col[:], func=ACT.Abs_reciprocal_sqrt, bias=floor_col[:], scale=1.0)
+        make_identity(nc, ident_bf[:])
+        make_identity(nc, ident_f[:])
+
+        g_abs = kept([P, 8], F32, "g_abs")
+        g_clamped = kept([P, 8], F32, "g_clamped")
+        ab = kept([P, 2, 8], F32, "ab")
+        rest1 = kept([P, 2, 8], F32, "rest1")
+        rest2 = kept([P, 2, 8], F32, "rest2")
+        g_sign = kept([P, 2, T], BF16, "g_sign")
+        d_lhs = kept([P, 8, P], BF16, "d_lhs")
+        g_flat = g_sb[:].rearrange("p a t -> p (a t)")
+        nv_flat = nv_sb[:].rearrange("p a t -> p (a t)")
+
+        def piece(n):
+            return pieces[:].rearrange("p s (c x) -> p c s x", c=4)[:, 0:2, :, n]
+
+        small = [
+            lambda: nc.vector.scalar_tensor_tensor(out=g_abs[:], in0=g_flat, scalar=-1.0, in1=g_flat, op0=ALU.mult, op1=ALU.max),
+            lambda: nc.vector.tensor_scalar(out=g_clamped[:], in0=g_abs[:], scalar1=G_FLOOR, scalar2=1.0 / (ROOT_U * SHRINK_SIM), op0=ALU.max, op1=ALU.mult),
+            lambda: nc.vector.reciprocal(out=ab[:, 1, :], in_=g_clamped[:]),
+            lambda: nc.vector.scalar_tensor_tensor(out=ab[:, 0, :], in0=nv_flat, scalar=1.0 / SHRINK_SIM, in1=ab[:, 1, :], op0=ALU.mult, op1=ALU.mult),
+            lambda: nc.vector.tensor_copy(out=piece(0), in_=ab[:]),
+            lambda: nc.vector.tensor_tensor(out=rest1[:], in0=ab[:], in1=piece(0), op=ALU.subtract),
+            lambda: nc.vector.tensor_copy(out=piece(1), in_=rest1[:]),
+            lambda: nc.vector.tensor_tensor(out=rest2[:], in0=rest1[:], in1=piece(1), op=ALU.subtract),
+            lambda: nc.vector.tensor_copy(out=piece(2), in_=rest2[:]),
+        ]
+
+        def small_step():
+            small.pop(0)()
+
+        def turn_pieces():
+            bank = side_bank([P, 8, P], BF16)
+            for s in range(8):
+                nc.tensor.transpose(bank[:, s, :], pieces[:, s, :], ident_bf[:])
+            return bank
+
+        v_wide, v_il, v_mx = {}, {}, {}
+
+        def widen(a, half, t, on_scalar):
+            if (a, half) not in v_wide:
+                v_wide[a, half] = kept([P, T, KP], BF16, "v_wide_%d_%d" % (a, half))
+            src = v_raw[a, half][:, t, :].bitcast(FP8)
+            dst = v_wide[a, half][:, t, :]
+            if on_scalar:
+                nc.scalar.activation(out=dst, in_=src, func=ACT.Copy, scale=vs[:, a, t:t + 1])
+            else:
+                nc.vector.tensor_scalar(out=dst, in0=src, scalar1=vs[:, a, t:t + 1], scalar2=None, op0=ALU.mult)
+
+        def weave_v(a, half):
+            v_il[a, half] = work.tile([P, T * KP], BF16, name="v_il", tag="v_il", bufs=2, align_bytes=64)
+            nc.vector.tensor_copy(
+                out=v_il[a, half][:].rearrange("p (s m t) -> p m s t", s=T, t=T),
+                in_=v_wide[a, half][:].rearrange("p t (m s) -> p m s t", s=T))
+
+        def quantize(src, codes, scales):
+            nc.vector.quantize_mx(out=codes.bitcast(FP8X4), scales=scales, in_=src)
+
+        def quant_v(a, half):
+            v_mx[a, half] = mx_tiles(KP, "v_%d_%d" % (a, half))
+            quantize(v_il[a, half][:], v_mx[a, half][0][:], v_mx[a, half][1][:])
+
+        p_il, p_mx, p_bank = {}, {}, {}
+
+        def new_p_il(a, quarter):
+            p_il[a, quarter] = work.tile([P, 1024], BF16, name="p_il", tag="p_il", bufs=4, align_bytes=64)
+            return p_il[a, quarter]
+
+        def weave_p_pe(a, quarter):
+            bank = p_bank[a, quarter] = side_bank([P, 2, P, T], BF16)
+            for n in range(2):
+                nc.tensor.matmul(bank[:, n, :, :], lhsT=ident_bf[:],
+                                 rhs=p_raw[a, quarter][:, :, n * P:(n + 1) * P].rearrange("p t i -> p i t"),
+                                 start=True, stop=True)
+
+        def empty_p(a, quarter):
+            nc.scalar.copy(out=new_p_il(a, quarter)[:], in_=p_bank[a, quarter][:].rearrange("p n i t -> p (n i t)"))
+
+        def weave_p(a, quarter):
+            nc.vector.tensor_copy(out=new_p_il(a, quarter)[:].rearrange("p (i t) -> p i t", t=T),
+                                  in_=p_raw[a, quarter][:].rearrange("p t i -> p i t"))
+
+        def quant_p(a, quarter):
+            p_mx[a, quarter] = mx_tiles(256, "p_%d_%d" % (a, quarter))
+            quantize(p_il[a, quarter][:], p_mx[a, quarter][0][:], p_mx[a, quarter][1][:])
+
+        h_bank, h_il, h_mx = {}, {}, {}
+
+        def turn_h(pair, half):
+            bank = h_bank[pair, half] = side_bank([P, 2, 2, P], F32)
+            for r in range(2):
+                words = h_raw[pair][:, r, :].bitcast(F32)
+                for u in range(2):
+                    nc.tensor.transpose(bank[:, u, r, :], words[:, 256 * half + u:256 * (half + 1):2], ident_f[:])
+
+        def empty_h(pair, half):
+            h_il[pair, half] = work.tile([P, 1024], BF16, name="h_il", tag="h_il", bufs=3, align_bytes=64)
+            src = h_bank[pair, half][:].rearrange("p u r b -> p (u r b)").bitcast(BF16)
+            nc.vector.tensor_tensor(
+                out=h_il[pair, half][:].rearrange("p (b u e) -> p b u e", u=2, e=2),
+                in0=src.rearrange("p (u b e) -> p b u e", u=2, e=2),
+                in1=g_sign[:, half, :].rearrange("p (u e) -> p u e", u=2).unsqueeze(1).to_broadcast([P, 256, 2, 2]),
+                op=ALU.mult)
+
+        def quant_h(pair, half):
+            h_mx[pair, half] = mx_tiles(256, "h_%d_%d" % (pair, half))
+            quantize(h_il[pair, half][:], h_mx[pair, half][0][:], h_mx[pair, half][1][:])
+
+        c_bank, d_bank, w, z, den, y, y2, s_il, s_mx = {}, {}, {}, {}, {}, {}, {}, {}, {}
+
+        def cross(k):
+            chunk, half = BANKS[k]
+            cols = slice((chunk % 2) * P, (chunk % 2 + 1) * P)
+            c_bank[k] = psum.tile([P, T, P], F32, name="c_bank", tag="c_bank", bufs=4)
+            for t in range(T):
+                for a in range(2):
+                    v_codes, v_scales = v_mx[a, half]
+                    p_codes, p_scales = p_mx[a, chunk // 2]
+                    nc.tensor.matmul_mx(
+                        out=c_bank[k][:, t, :],
+                        lhsT=v_codes[:, t * P:(t + 1) * P].bitcast(FP8X4), lhsT_scale=v_scales[:, t * P:(t + 1) * P],
+                        rhs=p_codes[:, cols].bitcast(FP8X4), rhs_scale=p_scales[:, cols],
+                        start=(a == 0), stop=(a == 1))
+
+        def norms(k):
+            chunk, half = BANKS[k]
+            d_bank[k] = psum.tile([P, T, P], F32, name="d_bank", tag="d_bank", bufs=1)
+            for t in range(T):
+                nc.tensor.matmul(d_bank[k][:, t, :], lhsT=d_lhs[:, half * T + t, :], rhs=d_rhs[:, chunk * P:(chunk + 1) * P],
+                                 start=True, stop=True)
+
+        def f32_tile(tag):
+            return work.tile([P, P, T], F32, name=tag, tag=tag, bufs=2)
+
+        def do_w(k):
+            w[k] = f32_tile("w")
+            nc.scalar.activation(out=w[k][:], in_=c_bank[k][:].rearrange("p t i -> p i t"),
+                                 func=ACT.Abs_reciprocal_sqrt, bias=floor_col[:], scale=1.0 / DAMP)
+
+        def do_z(k):
+            z[k] = f32_tile("z")
+            nc.scalar.activation(out=z[k][:], in_=w[k][:], func=ACT.Square)
+
+        whole = slice(0, P)
+
+        def do_den(k, part=whole):
+            if k not in den:
+                den[k] = f32_tile("den")
+            nc.vector.scalar_tensor_tensor(out=den[k][:, part, :], in0=z[k][:, part, :], scalar=1.0,
+                                           in1=d_bank[k][:, :, part].rearrange("p t i -> p i t"), op0=ALU.add, op1=ALU.mult)
+
+        def do_y(k, part=whole):
+            if k not in y:
+                y[k] = f32_tile("y")
+            nc.scalar.activation(out=y[k][:, part, :], in_=den[k][:, part, :], func=ACT.Abs_reciprocal_sqrt)
+
+        def do_y2(k, part=whole):
+            if k not in y2:
+                y2[k] = f32_tile("y2")
+            nc.scalar.activation(out=y2[k][:, part, :], in_=y[k][:, part, :], func=ACT.Square)
+
+        def do_s(k, part=whole):
+            if k not in s_il:
+                s_il[k] = work.tile([P, P, T], BF16, name="s_il", tag="s_il", bufs=2, align_bytes=64)
+            nc.vector.tensor_tensor(out=s_il[k][:, part, :], in0=c_bank[k][:, :, part].rearrange("p t i -> p i t"),
+                                    in1=y2[k][:, part, :], op=ALU.mult)
+
+        def quant_s(k):
+            chunk, half = BANKS[k]
+            if (chunk // 2, half) not in s_mx:
+                s_mx[chunk // 2, half] = mx_tiles(256, "s_%d_%d" % (chunk // 2, half))
+            codes, scales = s_mx[chunk // 2, half]
+            cols = slice((chunk % 2) * P, (chunk % 2 + 1) * P)
+            quantize(s_il[k][:].rearrange("p i t -> p (i t)"), codes[:, cols], scales[:, cols])
+
+        o_bank = {}
+
+        def scores(i0, width, b0):
+            tiles = KP // width
+            bank = o_bank[i0, b0] = side_bank([P, tiles, width], F32)
+            cols = slice(i0 % 256, i0 % 256 + width)
+            for n in range(tiles):
+                bt = b0 + n
+                rows = slice((bt % 2) * P, (bt % 2 + 1) * P)
+                for half in range(2):
+                    h_codes, h_scales = h_mx[bt // 2, half]
+                    s_codes, s_scales = s_mx[i0 // 256, half]
+                    nc.tensor.matmul_mx(
+                        out=bank[:, n, :],
+                        lhsT=h_codes[:, rows].bitcast(FP8X4), lhsT_scale=h_scales[:, rows],
+                        rhs=s_codes[:, cols].bitcast(FP8X4), rhs_scale=s_scales[:, cols],
+                        start=(half == 0), stop=(half == 1))
+
+        def store(i0, width, b0, on_scalar):
+            tiles = KP // width
+            res = work.tile([P, tiles, width], F32, name="res", tag="res", bufs=6)
+            if on_scalar:
+                nc.scalar.copy(out=res[:], in_=o_bank[i0, b0][:])
+            else:
+                nc.vector.tensor_copy(out=res[:], in_=o_bank[i0, b0][:])
+            nc.sync.dma_start(out=out[b0 * P:(b0 + tiles) * P, i0:i0 + width].rearrange("(n p) i -> p n i", p=P), in_=res[:])
+
+        def score_pass(dst, bt, i0, width, half):
+            rows = slice((bt % 2) * P, (bt % 2 + 1) * P)
+            cols = slice(i0 % 256, i0 % 256 + width)
+            h_codes, h_scales = h_mx[bt // 2, half]
+            s_codes, s_scales = s_mx[i0 // 256, half]
+            nc.tensor.matmul_mx(
+                out=dst,
+                lhsT=h_codes[:, rows].bitcast(FP8X4), lhsT_scale=h_scales[:, rows],
+                rhs=s_codes[:, cols].bitcast(FP8X4), rhs_scale=s_scales[:, cols],
+                start=(half == 0), stop=(half == 1))
+
+        widen(0, 0, 0, False)
+        widen(0, 0, 2, True)
+        widen(0, 0, 1, False)
+        widen(0, 0, 3, True)
+        small_step()
+        small_step()
+        widen(1, 0, 0, False)
+        small_step()
+        widen(1, 0, 2, True)
+        widen(1, 0, 3, True)
+        weave_v(0, 0)
+        small_step()
+        widen(1, 0, 1, False)
+        small_step()
+        weave_p_pe(0, 0)
+        weave_p_pe(1, 0)
+        nc.scalar.activation(out=g_sign[:], in_=g_sb[:], func=ACT.Sign, bias=floor_col[:], scale=1.0)
+        empty_p(0, 0)
+        widen(0, 1, 0, True)
+        empty_p(1, 0)
+        weave_v(1, 0)
+        small_step()
+        quant_v(0, 0)
+        small_step()
+        quant_p(0, 0)
+        small_step()
+        quant_p(1, 0)
+        small_step()
+        quant_v(1, 0)
+        for t in range(1, T):
+            widen(0, 1, t, True)
+        for a in range(2):
+            weave_p_pe(a, 1)
+        pieces_bank = turn_pieces()
+        empty_p(0, 1)
+        nc.scalar.copy(out=d_lhs[:], in_=pieces_bank[:])
+        cross(0)
+        cross(1)
+        weave_v(0, 1)
+
+        vec_a = {
+            -1: [lambda: quant_p(0, 1), lambda: quant_v(0, 1), lambda: widen(1, 1, 0, False), lambda: widen(1, 1, 1, False), lambda: quant_p(1, 1)],
+            0: [lambda: weave_v(1, 1)],
+            1: [lambda: empty_h(0, 0)],
+            2: [lambda: empty_h(0, 1)],
+            3: [lambda: weave_p(0, 2)],
+            4: [lambda: weave_p(1, 2)],
+            5: [lambda: empty_h(1, 0)],
+            6: [lambda: empty_h(1, 1)],
+            7: [lambda: weave_p(0, 3)],
+            8: [lambda: weave_p(1, 3), lambda: empty_h(2, 0)],
+            9: [lambda: empty_h(2, 1), lambda: quant_h(2, 0)],
+            10: [lambda: empty_h(3, 0), lambda: store(256, 256, 2, False)],
+            11: [lambda: empty_h(3, 1), lambda: store(256, 256, 4, False)],
+            12: [lambda: store(512, 128, 0, False)],
+            13: [lambda: store(256, 256, 6, False), lambda: store(512, 128, 4, False)],
+            14: [lambda: store(640, 128, 0, False)],
+        }
+        vec_b = {
+            -1: [lambda: widen(1, 1, 2, False), lambda: widen(1, 1, 3, False)],
+            0: [lambda: quant_v(1, 1)],
+            1: [lambda: quant_h(0, 0)],
+            2: [lambda: quant_h(0, 1)],
+            3: [lambda: quant_p(0, 2)],
+            4: [lambda: quant_p(1, 2)],
+            5: [lambda: quant_h(1, 0)],
+            6: [lambda: quant_h(1, 1)],
+            7: [lambda: quant_p(0, 3)],
+            8: [lambda: quant_p(1, 3)],
+            9: [lambda: quant_h(2, 1)],
+            10: [lambda: quant_h(3, 0)],
+            11: [lambda: quant_h(3, 1)],
+            14: [lambda: store(640, 128, 4, False), lambda: scores(768, 128, 0), lambda: scores(768, 128, 4)],
+        }
+        act = {
+            -1: [lambda: empty_p(1, 1)],
+            8: [lambda: store(0, 256, 0, True)],
+            9: [lambda: store(0, 256, 2, True)],
+            10: [lambda: store(256, 256, 0, True)],
+            11: [lambda: store(0, 256, 4, True)],
+            13: [lambda: store(0, 256, 6, True)],
+        }
+        pe = {
+            0: [lambda: turn_h(0, 0)],
+            1: [lambda: turn_h(0, 1)],
+            4: [lambda: turn_h(1, 0)],
+            5: [lambda: turn_h(1, 1)],
+            7: [lambda: scores(0, 256, 0), lambda: turn_h(2, 0)],
+            8: [lambda: scores(0, 256, 2), lambda: turn_h(2, 1)],
+            9: [lambda: scores(256, 256, 0), lambda: scores(256, 256, 2), lambda: turn_h(3, 0)],
+            10: [lambda: scores(0, 256, 4), lambda: scores(256, 256, 4), lambda: turn_h(3, 1)],
+            11: [lambda: scores(512, 128, 0)],
+            12: [lambda: scores(0, 256, 6), lambda: scores(256, 256, 6), lambda: scores(512, 128, 4)],
+            13: [lambda: scores(640, 128, 0), lambda: scores(640, 128, 4)],
+        }
+        last = len(BANKS) - 1
+
+        def run(jobs, k):
+            for job in jobs.get(k, []):
+                job()
+
+        for k in range(-1, last):
+            if k + 1 <= last:
+                do_w(k + 1)
+            run(act, k)
+            run(vec_a, k)
+            if k + 1 <= last:
+                norms(k + 1)
+            if 2 <= k + 2 <= last:
+                cross(k + 2)
+            run(pe, k)
+            if 0 <= k - 1:
+                do_y2(k - 1)
+                do_s(k - 1)
+            if k + 1 <= last:
+                do_z(k + 1)
+                do_den(k + 1)
+            if 0 <= k <= last:
+                do_y(k)
+            if 0 <= k - 1:
+                quant_s(k - 1)
+            run(vec_b, k)
+        halves = [slice(0, P // 2), slice(P // 2, P)]
+        do_y2(last - 1)
+        do_s(last - 1)
+        for part in halves:
+            do_y(last, part)
+        for part in halves:
+            do_y2(last, part)
+        quant_s(last - 1)
+        for part in halves:
+            do_s(last, part)
+        store(768, 128, 0, True)
+        store(768, 128, 4, True)
+        tags = [("c_bank", 4), ("c_bank", 4), ("d_bank", 1), ("side", 3), ("c_bank", 4), ("side", 3), ("c_bank", 4), ("side", 3)]
+        tail = []
+        for bt, (tag, bufs) in enumerate(tags):
+            bank = psum.tile([P, P], F32, name=tag, tag=tag, bufs=bufs)
+            tail.append(bank)
+            score_pass(bank[:], bt, 896, P, 0)
+        quant_s(last)
+        for bt in range(8):
+            score_pass(tail[bt][:], bt, 896, P, 1)
+        for pair in range(4):
+            res = work.tile([P, 2, P], F32, name="res", tag="res", bufs=6)
+            nc.scalar.copy(out=res[:, 0, :], in_=tail[2 * pair][:])
+            nc.vector.tensor_copy(out=res[:, 1, :], in_=tail[2 * pair + 1][:])
+            nc.sync.dma_start(out=out[2 * pair * P:(2 * pair + 2) * P, 896:1024].rearrange("(n p) i -> p n i", p=P), in_=res[:])

@@ -63,9 +63,10 @@ def tile_crossoccurrencedampedscores_kernel(tc, p, v_bytes, v_scale, n_p, n_v, g
             v_raw[a, half] = kept([P, T, KP], U8, "v_raw_%d_%d" % (a, half))
             nc.sync.dma_start(out=v_raw[a, half][:], in_=v_rows[a][:, :, half * KP:(half + 1) * KP])
 
-        def load_p(a, quarter):
-            p_raw[a, quarter] = kept([P, T, 256], BF16, "p_raw_%d_%d" % (a, quarter))
-            nc.sync.dma_start(out=p_raw[a, quarter][:], in_=p_rows[a][:, :, quarter * 256:(quarter + 1) * 256])
+        def load_p(quarter):
+            p_raw[quarter] = kept([P, 2, T, 256], BF16, "p_raw_%d" % quarter)
+            for a in range(2):
+                nc.sync.dma_start(out=p_raw[quarter][:, a, :, :], in_=p_rows[a][:, :, quarter * 256:(quarter + 1) * 256])
 
         def load_h(pair):
             h_raw[pair] = kept([P, 2, J], BF16, "h_raw_%d" % pair)
@@ -75,19 +76,15 @@ def tile_crossoccurrencedampedscores_kernel(tc, p, v_bytes, v_scale, n_p, n_v, g
         nc.sync.dma_start(out=g_sb[:], in_=g.rearrange("(a p t) -> p a t", p=P, t=T))
         nc.sync.dma_start(out=nv_sb[:], in_=n_v.rearrange("(a p t) -> p a t", p=P, t=T))
         load_v(1, 0)
-        for a in range(2):
-            load_p(a, 0)
+        load_p(0)
         nc.sync.dma_start(out=d_rhs[0:4, :], in_=n_p.partition_broadcast(4))
         load_v(0, 1)
-        for a in range(2):
-            load_p(a, 1)
+        load_p(1)
         load_v(1, 1)
         load_h(0)
-        for a in range(2):
-            load_p(a, 2)
+        load_p(2)
         load_h(1)
-        for a in range(2):
-            load_p(a, 3)
+        load_p(3)
         load_h(2)
         load_h(3)
 
@@ -161,27 +158,29 @@ def tile_crossoccurrencedampedscores_kernel(tc, p, v_bytes, v_scale, n_p, n_v, g
 
         p_il, p_mx, p_bank = {}, {}, {}
 
-        def new_p_il(a, quarter):
-            p_il[a, quarter] = work.tile([P, 1024], BF16, name="p_il", tag="p_il", bufs=4, align_bytes=64)
-            return p_il[a, quarter]
+        def new_p_il(chunk):
+            p_il[chunk] = work.tile([P, 2 * KP], BF16, name="p_il", tag="p_il", bufs=3, align_bytes=64)
+            return p_il[chunk]
 
-        def weave_p_pe(a, quarter):
-            bank = p_bank[a, quarter] = side_bank([P, 2, P, T], BF16)
-            for n in range(2):
-                nc.tensor.matmul(bank[:, n, :, :], lhsT=ident_bf[:],
-                                 rhs=p_raw[a, quarter][:, :, n * P:(n + 1) * P].rearrange("p t i -> p i t"),
+        def p_chunk(chunk):
+            return p_raw[chunk // 2][:, :, :, (chunk % 2) * P:(chunk % 2 + 1) * P]
+
+        def weave_p_pe(chunk):
+            bank = p_bank[chunk] = side_bank([P, 2, P, T], BF16)
+            for a in range(2):
+                nc.tensor.matmul(bank[:, a, :, :], lhsT=ident_bf[:], rhs=p_chunk(chunk)[:, a, :, :].rearrange("p t i -> p i t"),
                                  start=True, stop=True)
 
-        def empty_p(a, quarter):
-            nc.scalar.copy(out=new_p_il(a, quarter)[:], in_=p_bank[a, quarter][:].rearrange("p n i t -> p (n i t)"))
+        def empty_p(chunk):
+            nc.scalar.copy(out=new_p_il(chunk)[:], in_=p_bank[chunk][:].rearrange("p a i t -> p (a i t)"))
 
-        def weave_p(a, quarter):
-            nc.vector.tensor_copy(out=new_p_il(a, quarter)[:].rearrange("p (i t) -> p i t", t=T),
-                                  in_=p_raw[a, quarter][:].rearrange("p t i -> p i t"))
+        def weave_p(chunk):
+            nc.vector.tensor_copy(out=new_p_il(chunk)[:].rearrange("p (a c i t) -> p a c t i", a=2, t=T, i=4),
+                                  in_=p_chunk(chunk).rearrange("p a t (c i) -> p a c t i", i=4))
 
-        def quant_p(a, quarter):
-            p_mx[a, quarter] = mx_tiles(256, "p_%d_%d" % (a, quarter))
-            quantize(p_il[a, quarter][:], p_mx[a, quarter][0][:], p_mx[a, quarter][1][:])
+        def quant_p(chunk):
+            p_mx[chunk] = mx_tiles(256, "p_%d" % chunk)
+            quantize(p_il[chunk][:], p_mx[chunk][0][:], p_mx[chunk][1][:])
 
         h_bank, h_il, h_mx = {}, {}, {}
 
@@ -209,12 +208,12 @@ def tile_crossoccurrencedampedscores_kernel(tc, p, v_bytes, v_scale, n_p, n_v, g
 
         def cross(k):
             chunk, half = BANKS[k]
-            cols = slice((chunk % 2) * P, (chunk % 2 + 1) * P)
             c_bank[k] = psum.tile([P, T, P], F32, name="c_bank", tag="c_bank", bufs=4)
             for t in range(T):
                 for a in range(2):
                     v_codes, v_scales = v_mx[a, half]
-                    p_codes, p_scales = p_mx[a, chunk // 2]
+                    p_codes, p_scales = p_mx[chunk]
+                    cols = slice(a * P, (a + 1) * P)
                     nc.tensor.matmul_mx(
                         out=c_bank[k][:, t, :],
                         lhsT=v_codes[:, t * P:(t + 1) * P].bitcast(FP8X4), lhsT_scale=v_scales[:, t * P:(t + 1) * P],
@@ -318,74 +317,73 @@ def tile_crossoccurrencedampedscores_kernel(tc, p, v_bytes, v_scale, n_p, n_v, g
         small_step()
         widen(1, 0, 0, False)
         small_step()
-        widen(1, 0, 2, True)
-        widen(1, 0, 3, True)
+        for t in range(1, T):
+            widen(1, 0, t, True)
         weave_v(0, 0)
         small_step()
-        widen(1, 0, 1, False)
-        small_step()
-        weave_p_pe(0, 0)
-        weave_p_pe(1, 0)
+        weave_p_pe(0)
+        weave_p_pe(1)
         nc.scalar.activation(out=g_sign[:], in_=g_sb[:], func=ACT.Sign, bias=floor_col[:], scale=1.0)
-        empty_p(0, 0)
-        widen(0, 1, 0, True)
-        empty_p(1, 0)
+        empty_p(0)
         weave_v(1, 0)
         small_step()
         quant_v(0, 0)
         small_step()
-        quant_p(0, 0)
-        small_step()
-        quant_p(1, 0)
+        quant_p(0)
         small_step()
         quant_v(1, 0)
-        for t in range(1, T):
+        small_step()
+        widen(0, 1, 0, True)
+        empty_p(1)
+        for t in range(1, T - 1):
             widen(0, 1, t, True)
-        for a in range(2):
-            weave_p_pe(a, 1)
-        pieces_bank = turn_pieces()
-        empty_p(0, 1)
-        nc.scalar.copy(out=d_lhs[:], in_=pieces_bank[:])
+        weave_p_pe(2)
         cross(0)
-        cross(1)
+        quant_p(1)
+        small_step()
+        pieces_bank = turn_pieces()
+        empty_p(2)
+        widen(0, 1, T - 1, False)
+        widen(1, 1, 0, False)
         weave_v(0, 1)
+        weave_p_pe(3)
 
         vec_a = {
-            -1: [lambda: quant_p(0, 1), lambda: quant_v(0, 1), lambda: widen(1, 1, 0, False), lambda: widen(1, 1, 1, False), lambda: quant_p(1, 1)],
-            0: [lambda: weave_v(1, 1)],
+            -1: [lambda: quant_p(2), lambda: quant_v(0, 1), lambda: widen(1, 1, 1, False), lambda: widen(1, 1, 2, False)],
+            0: [lambda: quant_p(3), lambda: weave_v(1, 1)],
             1: [lambda: empty_h(0, 0)],
             2: [lambda: empty_h(0, 1)],
-            3: [lambda: weave_p(0, 2)],
-            4: [lambda: weave_p(1, 2)],
-            5: [lambda: empty_h(1, 0)],
-            6: [lambda: empty_h(1, 1)],
-            7: [lambda: weave_p(0, 3)],
-            8: [lambda: weave_p(1, 3), lambda: empty_h(2, 0)],
-            9: [lambda: empty_h(2, 1), lambda: quant_h(2, 0)],
-            10: [lambda: empty_h(3, 0), lambda: store(256, 256, 2, False)],
-            11: [lambda: empty_h(3, 1), lambda: store(256, 256, 4, False)],
+            3: [lambda: empty_h(1, 0)],
+            4: [lambda: weave_p(4)],
+            5: [lambda: empty_h(1, 1)],
+            6: [lambda: weave_p(5)],
+            7: [lambda: empty_h(2, 0)],
+            8: [lambda: weave_p(6), lambda: empty_h(2, 1)],
+            9: [lambda: empty_h(3, 0), lambda: quant_h(2, 1)],
+            10: [lambda: empty_h(3, 1), lambda: weave_p(7)],
+            11: [lambda: store(256, 256, 2, False), lambda: store(256, 256, 4, False)],
             12: [lambda: store(512, 128, 0, False)],
             13: [lambda: store(256, 256, 6, False), lambda: store(512, 128, 4, False)],
             14: [lambda: store(640, 128, 0, False)],
         }
         vec_b = {
-            -1: [lambda: widen(1, 1, 2, False), lambda: widen(1, 1, 3, False)],
+            -1: [lambda: widen(1, 1, 3, False)],
             0: [lambda: quant_v(1, 1)],
             1: [lambda: quant_h(0, 0)],
             2: [lambda: quant_h(0, 1)],
-            3: [lambda: quant_p(0, 2)],
-            4: [lambda: quant_p(1, 2)],
-            5: [lambda: quant_h(1, 0)],
-            6: [lambda: quant_h(1, 1)],
-            7: [lambda: quant_p(0, 3)],
-            8: [lambda: quant_p(1, 3)],
-            9: [lambda: quant_h(2, 1)],
-            10: [lambda: quant_h(3, 0)],
-            11: [lambda: quant_h(3, 1)],
+            3: [lambda: quant_h(1, 0)],
+            4: [lambda: quant_p(4)],
+            5: [lambda: quant_h(1, 1)],
+            6: [lambda: quant_p(5)],
+            7: [lambda: quant_h(2, 0)],
+            8: [lambda: quant_p(6)],
+            9: [lambda: quant_h(3, 0)],
+            10: [lambda: quant_h(3, 1), lambda: quant_p(7)],
             14: [lambda: store(640, 128, 4, False), lambda: scores(768, 128, 0), lambda: scores(768, 128, 4)],
         }
         act = {
-            -1: [lambda: empty_p(1, 1)],
+            -1: [lambda: nc.scalar.copy(out=d_lhs[:], in_=pieces_bank[:])],
+            0: [lambda: empty_p(3)],
             8: [lambda: store(0, 256, 0, True)],
             9: [lambda: store(0, 256, 2, True)],
             10: [lambda: store(256, 256, 0, True)],
@@ -395,15 +393,17 @@ def tile_crossoccurrencedampedscores_kernel(tc, p, v_bytes, v_scale, n_p, n_v, g
         pe = {
             0: [lambda: turn_h(0, 0)],
             1: [lambda: turn_h(0, 1)],
-            4: [lambda: turn_h(1, 0)],
-            5: [lambda: turn_h(1, 1)],
-            7: [lambda: scores(0, 256, 0), lambda: turn_h(2, 0)],
-            8: [lambda: scores(0, 256, 2), lambda: turn_h(2, 1)],
-            9: [lambda: scores(256, 256, 0), lambda: scores(256, 256, 2), lambda: turn_h(3, 0)],
-            10: [lambda: scores(0, 256, 4), lambda: scores(256, 256, 4), lambda: turn_h(3, 1)],
+            2: [lambda: turn_h(1, 0)],
+            4: [lambda: turn_h(1, 1)],
+            6: [lambda: turn_h(2, 0)],
+            7: [lambda: scores(0, 256, 0), lambda: turn_h(2, 1)],
+            8: [lambda: scores(0, 256, 2), lambda: turn_h(3, 0)],
+            9: [lambda: scores(256, 256, 0), lambda: turn_h(3, 1)],
+            10: [lambda: scores(0, 256, 4), lambda: scores(256, 256, 2), lambda: scores(256, 256, 4)],
             11: [lambda: scores(512, 128, 0)],
             12: [lambda: scores(0, 256, 6), lambda: scores(256, 256, 6), lambda: scores(512, 128, 4)],
-            13: [lambda: scores(640, 128, 0), lambda: scores(640, 128, 4)],
+            13: [lambda: scores(640, 128, 0)],
+            14: [lambda: scores(640, 128, 4)],
         }
         last = len(BANKS) - 1
 
@@ -412,14 +412,12 @@ def tile_crossoccurrencedampedscores_kernel(tc, p, v_bytes, v_scale, n_p, n_v, g
                 job()
 
         for k in range(-1, last):
-            if k + 1 <= last:
-                do_w(k + 1)
+            do_w(k + 1)
             run(act, k)
-            run(vec_a, k)
-            if k + 1 <= last:
-                norms(k + 1)
-            if 2 <= k + 2 <= last:
+            if k + 2 <= last:
                 cross(k + 2)
+            run(vec_a, k)
+            norms(k + 1)
             run(pe, k)
             if 0 <= k - 1:
                 do_y2(k - 1)
@@ -444,15 +442,19 @@ def tile_crossoccurrencedampedscores_kernel(tc, p, v_bytes, v_scale, n_p, n_v, g
             do_s(last, part)
         store(768, 128, 0, True)
         store(768, 128, 4, True)
-        tags = [("c_bank", 4), ("c_bank", 4), ("d_bank", 1), ("side", 3), ("c_bank", 4), ("side", 3), ("c_bank", 4), ("side", 3)]
+        tags = [("c_bank", 4), ("c_bank", 4), ("d_bank", 1), ("side", 3), ("c_bank", 4), ("side", 3), ("c_bank", 4)]
         tail = []
         for bt, (tag, bufs) in enumerate(tags):
             bank = psum.tile([P, P], F32, name=tag, tag=tag, bufs=bufs)
             tail.append(bank)
             score_pass(bank[:], bt, 896, P, 0)
         quant_s(last)
-        for bt in range(8):
+        for bt in range(7):
             score_pass(tail[bt][:], bt, 896, P, 1)
+        bank = side_bank([P, P], F32)
+        tail.append(bank)
+        for half in range(2):
+            score_pass(bank[:], 7, 896, P, half)
         for pair in range(4):
             res = work.tile([P, 2, P], F32, name="res", tag="res", bufs=6)
             nc.scalar.copy(out=res[:, 0, :], in_=tail[2 * pair][:])

@@ -18,40 +18,93 @@ ALU = mybir.AluOpType
 P = 128
 T = 4
 KP = P * T
+WIDE = 2 * P
+CHUNKS = I // P
 ROOT_U = 32.0
 SHRINK_SIM = 0.5
 SHRINK_DAMP = 0.5
 DAMP = ROOT_U * SHRINK_DAMP
 C_FLOOR = 2.0 ** -60
 G_FLOOR = 2.0 ** -50
+PIECES = 3
+ONES_ROW = 32
 
-BANKS = [(c, half) for half in range(2) for c in range(4)] + [(c, half) for c in range(4, 8) for half in range(2)]
+C_BANKS, D_BANKS, SIDE_BANKS = 4, 1, 3
+
+EARLY = 4
+BANKS = ([(chunk, half) for half in range(2) for chunk in range(EARLY)]
+         + [(chunk, half) for chunk in range(EARLY, CHUNKS) for half in range(2)])
+LAST = len(BANKS) - 1
+
+FIRST_COPY_STEP = 8
+LAST_SCALAR_COPY_STEP = 11
+
+
+def plan_operands():
+    p_step = {chunk: BANKS.index((chunk, 0)) - 4 for chunk in range(EARLY, CHUNKS)}
+    free = [k for k in range(1, LAST) if k >= FIRST_COPY_STEP or k not in p_step.values()]
+    h_step = dict(zip([(pair, half) for pair in range(B // WIDE) for half in range(2)], free))
+    return p_step, h_step
+
+
+def plan_outputs(h_step):
+    banks = [(i0, WIDE, b0) for i0 in range(0, EARLY * P, WIDE) for b0 in range(0, B // P, 2)]
+    banks = banks + [(chunk * P, P, b0) for chunk in range(EARLY, CHUNKS - 2) for b0 in range(0, B // P, T)]
+
+    def ready(bank):
+        i0, items, b0 = bank
+        s_done = BANKS.index(((i0 + items) // P - 1, 1)) + 1
+        h_done = h_step[(b0 + KP // items - 1) // 2, 1]
+        return max(s_done, h_done) + 1
+
+    waiting = sorted(banks, key=ready)
+    by_step = {}
+    for k in range(LAST):
+        room = 1 if k < max(h_step.values()) else 2
+        by_step[k] = [bank for bank in waiting[:room] if ready(bank) <= k]
+        waiting = waiting[len(by_step[k]):]
+    assert not waiting
+    return by_step
 
 
 def tile_crossoccurrencedampedscores_kernel(tc, p, v_bytes, v_scale, n_p, n_v, g, h, out):
     nc = tc.nc
     with ExitStack() as ctx:
         keep = ctx.enter_context(tc.tile_pool(name="keep", bufs=1))
-        work = ctx.enter_context(tc.tile_pool(name="work", bufs=3))
+        work = ctx.enter_context(tc.tile_pool(name="work", bufs=2))
         psum = ctx.enter_context(tc.psum_pool(name="psum", bufs=1))
         ctx.enter_context(tc.manual_schedule())
 
         def kept(shape, dtype, name):
             return keep.tile(shape, dtype, name=name, align_bytes=64)
 
-        def mx_tiles(width, name):
-            return kept([P, width], U32, name + "_codes"), kept([P, width], U8, name + "_scales")
+        def mx_tiles(words, name):
+            return kept([P, words], U32, name + "_codes"), kept([P, words], U8, name + "_scales")
 
-        def side_bank(shape, dtype):
-            return psum.tile(shape, dtype, name="side", tag="side", bufs=3)
+        def bank_tile(tag, shape, dtype=F32):
+            bufs = {"c": C_BANKS, "d": D_BANKS, "side": SIDE_BANKS}[tag]
+            return psum.tile(shape, dtype, name=tag + "_bank", tag=tag, bufs=bufs)
+
+        def quantize(woven, codes, scales):
+            nc.vector.quantize_mx(out=codes.bitcast(FP8X4), scales=scales, in_=woven)
+
+        def mx_pass(dst, stationary, m_cols, moving, n_cols, first):
+            nc.tensor.matmul_mx(
+                out=dst,
+                lhsT=stationary[0][:, m_cols].bitcast(FP8X4), lhsT_scale=stationary[1][:, m_cols],
+                rhs=moving[0][:, n_cols].bitcast(FP8X4), rhs_scale=moving[1][:, n_cols],
+                start=first, stop=not first)
+
+        def span(n, width=P):
+            return slice(n * width, (n + 1) * width)
 
         vs = kept([P, 2, T], F32, "vs")
         g_sb = kept([P, 2, T], BF16, "g_sb")
         nv_sb = kept([P, 2, T], BF16, "nv_sb")
-        d_rhs = kept([P, I], BF16, "d_rhs")
+        d_moving = kept([P, I], BF16, "d_moving")
         floor_col = kept([P, 1], F32, "floor_col")
         nc.vector.memset(floor_col[:], C_FLOOR)
-        nc.vector.memset(d_rhs[:], 1.0)
+        nc.vector.memset(d_moving[:], 1.0)
         nc.scalar.dma_start(out=vs[:], in_=v_scale.rearrange("(a p t) o -> p a (t o)", p=P, t=T))
 
         v_rows = v_bytes.rearrange("(a p t) j -> a p t j", p=P, t=T)
@@ -61,12 +114,12 @@ def tile_crossoccurrencedampedscores_kernel(tc, p, v_bytes, v_scale, n_p, n_v, g
 
         def load_v(a, half):
             v_raw[a, half] = kept([P, T, KP], U8, "v_raw_%d_%d" % (a, half))
-            nc.sync.dma_start(out=v_raw[a, half][:], in_=v_rows[a][:, :, half * KP:(half + 1) * KP])
+            nc.sync.dma_start(out=v_raw[a, half][:], in_=v_rows[a][:, :, span(half, KP)])
 
         def load_p(quarter):
-            p_raw[quarter] = kept([P, 2, T, 256], BF16, "p_raw_%d" % quarter)
+            p_raw[quarter] = kept([P, 2, T, WIDE], BF16, "p_raw_%d" % quarter)
             for a in range(2):
-                nc.sync.dma_start(out=p_raw[quarter][:, a, :, :], in_=p_rows[a][:, :, quarter * 256:(quarter + 1) * 256])
+                nc.sync.dma_start(out=p_raw[quarter][:, a, :, :], in_=p_rows[a][:, :, span(quarter, WIDE)])
 
         def load_h(pair):
             h_raw[pair] = kept([P, 2, J], BF16, "h_raw_%d" % pair)
@@ -77,386 +130,325 @@ def tile_crossoccurrencedampedscores_kernel(tc, p, v_bytes, v_scale, n_p, n_v, g
         nc.sync.dma_start(out=nv_sb[:], in_=n_v.rearrange("(a p t) -> p a t", p=P, t=T))
         load_v(1, 0)
         load_p(0)
-        nc.sync.dma_start(out=d_rhs[0:4, :], in_=n_p.partition_broadcast(4))
+        nc.sync.dma_start(out=d_moving[0:4, :], in_=n_p.partition_broadcast(4))
         load_v(0, 1)
         load_p(1)
         load_v(1, 1)
-        load_h(0)
-        load_p(2)
-        load_h(1)
-        load_p(3)
+        for n in range(2):
+            load_h(n)
+            load_p(2 + n)
         load_h(2)
         load_h(3)
 
         ident_bf = kept([P, P], BF16, "ident_bf")
-        ident_f = kept([P, P], F32, "ident_f")
-        table_probe = kept([P, 1], F32, "table_probe")
-        pieces = kept([P, 8, P], BF16, "pieces")
+        ident_f32 = kept([P, P], F32, "ident_f32")
+        table_warm = kept([P, 1], F32, "table_warm")
+        pieces = kept([P, 2 * T, P], BF16, "pieces")
         nc.vector.memset(pieces[:], 0.0)
-        nc.scalar.activation(out=table_probe[:], in_=floor_col[:], func=ACT.Abs_reciprocal_sqrt, bias=floor_col[:], scale=1.0)
+        nc.scalar.activation(out=table_warm[:], in_=floor_col[:], func=ACT.Abs_reciprocal_sqrt, bias=floor_col[:], scale=1.0)
         make_identity(nc, ident_bf[:])
-        make_identity(nc, ident_f[:])
+        make_identity(nc, ident_f32[:])
 
-        g_abs = kept([P, 8], F32, "g_abs")
-        g_clamped = kept([P, 8], F32, "g_clamped")
-        ab = kept([P, 2, 8], F32, "ab")
-        rest1 = kept([P, 2, 8], F32, "rest1")
-        rest2 = kept([P, 2, 8], F32, "rest2")
+        g_abs = kept([P, 2 * T], F32, "g_abs")
+        g_bounded = kept([P, 2 * T], F32, "g_bounded")
+        rest = [kept([P, 2, 2 * T], F32, "rest_%d" % n) for n in range(PIECES)]
         g_sign = kept([P, 2, T], BF16, "g_sign")
-        d_lhs = kept([P, 8, P], BF16, "d_lhs")
+        d_stationary = kept([P, 2 * T, P], BF16, "d_stationary")
         g_flat = g_sb[:].rearrange("p a t -> p (a t)")
         nv_flat = nv_sb[:].rearrange("p a t -> p (a t)")
 
         def piece(n):
-            return pieces[:].rearrange("p s (c x) -> p c s x", c=4)[:, 0:2, :, n]
+            return pieces[:].rearrange("p s (f x) -> p f s x", x=ONES_ROW)[:, 0:2, :, n]
 
-        small = [
-            lambda: nc.vector.scalar_tensor_tensor(out=g_abs[:], in0=g_flat, scalar=-1.0, in1=g_flat, op0=ALU.mult, op1=ALU.max),
-            lambda: nc.vector.tensor_scalar(out=g_clamped[:], in0=g_abs[:], scalar1=G_FLOOR, scalar2=1.0 / (ROOT_U * SHRINK_SIM), op0=ALU.max, op1=ALU.mult),
-            lambda: nc.vector.reciprocal(out=ab[:, 1, :], in_=g_clamped[:]),
-            lambda: nc.vector.scalar_tensor_tensor(out=ab[:, 0, :], in0=nv_flat, scalar=1.0 / SHRINK_SIM, in1=ab[:, 1, :], op0=ALU.mult, op1=ALU.mult),
-            lambda: nc.vector.tensor_copy(out=piece(0), in_=ab[:]),
-            lambda: nc.vector.tensor_tensor(out=rest1[:], in0=ab[:], in1=piece(0), op=ALU.subtract),
-            lambda: nc.vector.tensor_copy(out=piece(1), in_=rest1[:]),
-            lambda: nc.vector.tensor_tensor(out=rest2[:], in0=rest1[:], in1=piece(1), op=ALU.subtract),
-            lambda: nc.vector.tensor_copy(out=piece(2), in_=rest2[:]),
+        factor_steps = [
+            lambda: nc.vector.scalar_tensor_tensor(out=g_abs[:], in0=g_flat, scalar=-1.0, in1=g_flat,
+                                                   op0=ALU.mult, op1=ALU.max),
+            lambda: nc.vector.tensor_scalar(out=g_bounded[:], in0=g_abs[:], scalar1=G_FLOOR,
+                                            scalar2=1.0 / (ROOT_U * SHRINK_SIM), op0=ALU.max, op1=ALU.mult),
+            lambda: nc.vector.reciprocal(out=rest[0][:, 1, :], in_=g_bounded[:]),
+            lambda: nc.vector.scalar_tensor_tensor(out=rest[0][:, 0, :], in0=nv_flat, scalar=1.0 / SHRINK_SIM,
+                                                   in1=rest[0][:, 1, :], op0=ALU.mult, op1=ALU.mult),
         ]
+        for n in range(PIECES):
+            factor_steps.append(lambda n=n: nc.vector.tensor_copy(out=piece(n), in_=rest[n][:]))
+            if n + 1 < PIECES:
+                factor_steps.append(lambda n=n: nc.vector.tensor_tensor(out=rest[n + 1][:], in0=rest[n][:],
+                                                                        in1=piece(n), op=ALU.subtract))
 
-        def small_step():
-            small.pop(0)()
+        def factor_step():
+            factor_steps.pop(0)()
 
         def turn_pieces():
-            bank = side_bank([P, 8, P], BF16)
-            for s in range(8):
+            bank = bank_tile("side", [P, 2 * T, P], BF16)
+            for s in range(2 * T):
                 nc.tensor.transpose(bank[:, s, :], pieces[:, s, :], ident_bf[:])
             return bank
 
-        v_wide, v_il, v_mx = {}, {}, {}
+        v_wide = {key: kept([P, T, KP], BF16, "v_wide_%d_%d" % key) for key in v_raw}
+        v_woven, v_mx = {}, {}
 
-        def widen(a, half, t, on_scalar):
-            if (a, half) not in v_wide:
-                v_wide[a, half] = kept([P, T, KP], BF16, "v_wide_%d_%d" % (a, half))
-            src = v_raw[a, half][:, t, :].bitcast(FP8)
-            dst = v_wide[a, half][:, t, :]
-            if on_scalar:
-                nc.scalar.activation(out=dst, in_=src, func=ACT.Copy, scale=vs[:, a, t:t + 1])
-            else:
-                nc.vector.tensor_scalar(out=dst, in0=src, scalar1=vs[:, a, t:t + 1], scalar2=None, op0=ALU.mult)
+        def widen_on_scalar(a, half, t):
+            nc.scalar.activation(out=v_wide[a, half][:, t, :], in_=v_raw[a, half][:, t, :].bitcast(FP8),
+                                 func=ACT.Copy, scale=vs[:, a, t:t + 1])
+
+        def widen_on_vector(a, half, t):
+            nc.vector.tensor_scalar(out=v_wide[a, half][:, t, :], in0=v_raw[a, half][:, t, :].bitcast(FP8),
+                                    scalar1=vs[:, a, t:t + 1], scalar2=None, op0=ALU.mult)
 
         def weave_v(a, half):
-            v_il[a, half] = work.tile([P, T * KP], BF16, name="v_il", tag="v_il", bufs=2, align_bytes=64)
+            v_woven[a, half] = work.tile([P, T * KP], BF16, name="v_woven", align_bytes=64)
             nc.vector.tensor_copy(
-                out=v_il[a, half][:].rearrange("p (s m t) -> p m s t", s=T, t=T),
-                in_=v_wide[a, half][:].rearrange("p t (m s) -> p m s t", s=T))
+                out=v_woven[a, half][:].rearrange("p (s m e t) -> p m s t e", s=T, t=T, e=2),
+                in_=v_wide[a, half][:].rearrange("p t (m e s) -> p m s t e", s=T, e=2))
 
-        def quantize(src, codes, scales):
-            nc.vector.quantize_mx(out=codes.bitcast(FP8X4), scales=scales, in_=src)
-
-        def quant_v(a, half):
+        def quantize_v(a, half):
             v_mx[a, half] = mx_tiles(KP, "v_%d_%d" % (a, half))
-            quantize(v_il[a, half][:], v_mx[a, half][0][:], v_mx[a, half][1][:])
+            quantize(v_woven[a, half][:], v_mx[a, half][0][:], v_mx[a, half][1][:])
 
-        p_il, p_mx, p_bank = {}, {}, {}
-
-        def new_p_il(chunk):
-            p_il[chunk] = work.tile([P, 2 * KP], BF16, name="p_il", tag="p_il", bufs=3, align_bytes=64)
-            return p_il[chunk]
+        p_bank, p_woven, p_mx = {}, {}, {}
 
         def p_chunk(chunk):
-            return p_raw[chunk // 2][:, :, :, (chunk % 2) * P:(chunk % 2 + 1) * P]
+            return p_raw[chunk // 2][:, :, :, span(chunk % 2)]
 
-        def weave_p_pe(chunk):
-            bank = p_bank[chunk] = side_bank([P, 2, P, T], BF16)
+        def new_p_woven(chunk):
+            p_woven[chunk] = work.tile([P, 2 * KP], BF16, name="p_woven", bufs=3, align_bytes=64)
+            return p_woven[chunk]
+
+        def weave_p_on_tensor(chunk):
+            p_bank[chunk] = bank_tile("side", [P, 2, P, T], BF16)
             for a in range(2):
-                nc.tensor.matmul(bank[:, a, :, :], lhsT=ident_bf[:], rhs=p_chunk(chunk)[:, a, :, :].rearrange("p t i -> p i t"),
-                                 start=True, stop=True)
+                nc.tensor.matmul(p_bank[chunk][:, a, :, :], lhsT=ident_bf[:],
+                                 rhs=p_chunk(chunk)[:, a, :, :].rearrange("p t i -> p i t"), start=True, stop=True)
 
         def empty_p(chunk):
-            nc.scalar.copy(out=new_p_il(chunk)[:], in_=p_bank[chunk][:].rearrange("p a i t -> p (a i t)"))
+            nc.scalar.copy(out=new_p_woven(chunk)[:], in_=p_bank[chunk][:].rearrange("p a i t -> p (a i t)"))
 
-        def weave_p(chunk):
-            nc.vector.tensor_copy(out=new_p_il(chunk)[:].rearrange("p (a c i t) -> p a c t i", a=2, t=T, i=4),
-                                  in_=p_chunk(chunk).rearrange("p a t (c i) -> p a c t i", i=4))
+        def weave_p_on_vector(chunk):
+            nc.vector.tensor_copy(out=new_p_woven(chunk)[:].rearrange("p (a c e t) -> p a c t e", a=2, t=T, e=4),
+                                  in_=p_chunk(chunk).rearrange("p a t (c e) -> p a c t e", e=4))
 
-        def quant_p(chunk):
-            p_mx[chunk] = mx_tiles(256, "p_%d" % chunk)
-            quantize(p_il[chunk][:], p_mx[chunk][0][:], p_mx[chunk][1][:])
+        def quantize_p(chunk):
+            p_mx[chunk] = mx_tiles(WIDE, "p_%d" % chunk)
+            quantize(p_woven[chunk][:], p_mx[chunk][0][:], p_mx[chunk][1][:])
 
-        h_bank, h_il, h_mx = {}, {}, {}
+        h_bank, h_woven, h_mx = {}, {}, {}
 
         def turn_h(pair, half):
-            bank = h_bank[pair, half] = side_bank([P, 2, 2, P], F32)
+            h_bank[pair, half] = bank_tile("side", [P, 2, 2, P])
             for r in range(2):
                 words = h_raw[pair][:, r, :].bitcast(F32)
                 for u in range(2):
-                    nc.tensor.transpose(bank[:, u, r, :], words[:, 256 * half + u:256 * (half + 1):2], ident_f[:])
+                    nc.tensor.transpose(h_bank[pair, half][:, u, r, :],
+                                        words[:, WIDE * half + u:WIDE * (half + 1):2], ident_f32[:])
 
         def empty_h(pair, half):
-            h_il[pair, half] = work.tile([P, 1024], BF16, name="h_il", tag="h_il", bufs=3, align_bytes=64)
-            src = h_bank[pair, half][:].rearrange("p u r b -> p (u r b)").bitcast(BF16)
+            h_woven[pair, half] = work.tile([P, WIDE * T], BF16, name="h_woven", bufs=3, align_bytes=64)
+            turned = h_bank[pair, half][:].rearrange("p u r b -> p (u r b)").bitcast(BF16)
+            signs = g_sign[:, half, :].rearrange("p (u e) -> p u e", u=2).unsqueeze(1)
             nc.vector.tensor_tensor(
-                out=h_il[pair, half][:].rearrange("p (b u e) -> p b u e", u=2, e=2),
-                in0=src.rearrange("p (u b e) -> p b u e", u=2, e=2),
-                in1=g_sign[:, half, :].rearrange("p (u e) -> p u e", u=2).unsqueeze(1).to_broadcast([P, 256, 2, 2]),
-                op=ALU.mult)
+                out=h_woven[pair, half][:].rearrange("p (b u e) -> p b u e", u=2, e=2),
+                in0=turned.rearrange("p (u b e) -> p b u e", u=2, e=2),
+                in1=signs.to_broadcast([P, WIDE, 2, 2]), op=ALU.mult)
 
-        def quant_h(pair, half):
-            h_mx[pair, half] = mx_tiles(256, "h_%d_%d" % (pair, half))
-            quantize(h_il[pair, half][:], h_mx[pair, half][0][:], h_mx[pair, half][1][:])
+        def quantize_h(pair, half):
+            h_mx[pair, half] = mx_tiles(WIDE, "h_%d_%d" % (pair, half))
+            quantize(h_woven[pair, half][:], h_mx[pair, half][0][:], h_mx[pair, half][1][:])
 
-        c_bank, d_bank, w, z, den, y, y2, s_il, s_mx = {}, {}, {}, {}, {}, {}, {}, {}, {}
+        c_bank, d_bank, root, ratio, den, den_root, recip, s_woven, s_mx = {}, {}, {}, {}, {}, {}, {}, {}, {}
+        whole = slice(0, P // 2)
+
+        def chain_tile(tiles, k, name):
+            if k not in tiles:
+                tiles[k] = work.tile([P, P // 2, T * 2], F32, name=name)
+            return tiles[k]
+
+        def c_pairs(k):
+            return c_bank[k][:].rearrange("p t (c e) -> p c t e", e=2)
 
         def cross(k):
             chunk, half = BANKS[k]
-            c_bank[k] = psum.tile([P, T, P], F32, name="c_bank", tag="c_bank", bufs=4)
+            c_bank[k] = bank_tile("c", [P, T, P])
             for t in range(T):
                 for a in range(2):
-                    v_codes, v_scales = v_mx[a, half]
-                    p_codes, p_scales = p_mx[chunk]
-                    cols = slice(a * P, (a + 1) * P)
-                    nc.tensor.matmul_mx(
-                        out=c_bank[k][:, t, :],
-                        lhsT=v_codes[:, t * P:(t + 1) * P].bitcast(FP8X4), lhsT_scale=v_scales[:, t * P:(t + 1) * P],
-                        rhs=p_codes[:, cols].bitcast(FP8X4), rhs_scale=p_scales[:, cols],
-                        start=(a == 0), stop=(a == 1))
+                    mx_pass(c_bank[k][:, t, :], v_mx[a, half], span(t), p_mx[chunk], span(a), a == 0)
 
         def norms(k):
             chunk, half = BANKS[k]
-            d_bank[k] = psum.tile([P, T, P], F32, name="d_bank", tag="d_bank", bufs=1)
+            d_bank[k] = bank_tile("d", [P, P // 2, T, 2])
             for t in range(T):
-                nc.tensor.matmul(d_bank[k][:, t, :], lhsT=d_lhs[:, half * T + t, :], rhs=d_rhs[:, chunk * P:(chunk + 1) * P],
+                nc.tensor.matmul(d_bank[k][:, :, t, :], lhsT=d_stationary[:, half * T + t, :],
+                                 rhs=d_moving[:, span(chunk)].rearrange("p (c e) -> p c e", e=2),
                                  start=True, stop=True)
 
-        def f32_tile(tag):
-            return work.tile([P, P, T], F32, name=tag, tag=tag, bufs=2)
+        def take_root(k):
+            nc.scalar.activation(out=chain_tile(root, k, "root")[:].rearrange("p c (t e) -> p c t e", e=2),
+                                 in_=c_pairs(k), func=ACT.Abs_reciprocal_sqrt, bias=floor_col[:], scale=1.0 / DAMP)
 
-        def do_w(k):
-            w[k] = f32_tile("w")
-            nc.scalar.activation(out=w[k][:], in_=c_bank[k][:].rearrange("p t i -> p i t"),
-                                 func=ACT.Abs_reciprocal_sqrt, bias=floor_col[:], scale=1.0 / DAMP)
+        def take_ratio(k):
+            nc.scalar.activation(out=chain_tile(ratio, k, "ratio")[:], in_=root[k][:], func=ACT.Square)
 
-        def do_z(k):
-            z[k] = f32_tile("z")
-            nc.scalar.activation(out=z[k][:], in_=w[k][:], func=ACT.Square)
+        def take_den(k):
+            nc.vector.scalar_tensor_tensor(out=chain_tile(den, k, "den")[:], in0=ratio[k][:], scalar=1.0,
+                                           in1=d_bank[k][:].rearrange("p c t e -> p c (t e)"),
+                                           op0=ALU.add, op1=ALU.mult)
 
-        whole = slice(0, P)
+        def take_den_root(k, part=whole):
+            nc.scalar.activation(out=chain_tile(den_root, k, "den_root")[:, part, :], in_=den[k][:, part, :],
+                                 func=ACT.Abs_reciprocal_sqrt)
 
-        def do_den(k, part=whole):
-            if k not in den:
-                den[k] = f32_tile("den")
-            nc.vector.scalar_tensor_tensor(out=den[k][:, part, :], in0=z[k][:, part, :], scalar=1.0,
-                                           in1=d_bank[k][:, :, part].rearrange("p t i -> p i t"), op0=ALU.add, op1=ALU.mult)
+        def take_recip(k, part=whole):
+            nc.scalar.activation(out=chain_tile(recip, k, "recip")[:, part, :], in_=den_root[k][:, part, :],
+                                 func=ACT.Square)
 
-        def do_y(k, part=whole):
-            if k not in y:
-                y[k] = f32_tile("y")
-            nc.scalar.activation(out=y[k][:, part, :], in_=den[k][:, part, :], func=ACT.Abs_reciprocal_sqrt)
+        def take_s(k, part=whole):
+            if k not in s_woven:
+                s_woven[k] = work.tile([P, P, T], BF16, name="s_woven", align_bytes=64)
+            nc.vector.tensor_tensor(
+                out=s_woven[k][:].rearrange("p (c e) t -> p c t e", e=2)[:, part, :, :], in0=c_pairs(k)[:, part, :, :],
+                in1=recip[k][:, part, :].rearrange("p c (t e) -> p c t e", e=2), op=ALU.mult)
 
-        def do_y2(k, part=whole):
-            if k not in y2:
-                y2[k] = f32_tile("y2")
-            nc.scalar.activation(out=y2[k][:, part, :], in_=y[k][:, part, :], func=ACT.Square)
-
-        def do_s(k, part=whole):
-            if k not in s_il:
-                s_il[k] = work.tile([P, P, T], BF16, name="s_il", tag="s_il", bufs=2, align_bytes=64)
-            nc.vector.tensor_tensor(out=s_il[k][:, part, :], in0=c_bank[k][:, :, part].rearrange("p t i -> p i t"),
-                                    in1=y2[k][:, part, :], op=ALU.mult)
-
-        def quant_s(k):
+        def quantize_s(k):
             chunk, half = BANKS[k]
             if (chunk // 2, half) not in s_mx:
-                s_mx[chunk // 2, half] = mx_tiles(256, "s_%d_%d" % (chunk // 2, half))
+                s_mx[chunk // 2, half] = mx_tiles(WIDE, "s_%d_%d" % (chunk // 2, half))
             codes, scales = s_mx[chunk // 2, half]
-            cols = slice((chunk % 2) * P, (chunk % 2 + 1) * P)
-            quantize(s_il[k][:].rearrange("p i t -> p (i t)"), codes[:, cols], scales[:, cols])
+            quantize(s_woven[k][:].rearrange("p i t -> p (i t)"), codes[:, span(chunk % 2)], scales[:, span(chunk % 2)])
 
         o_bank = {}
 
-        def scores(i0, width, b0):
-            tiles = KP // width
-            bank = o_bank[i0, b0] = side_bank([P, tiles, width], F32)
-            cols = slice(i0 % 256, i0 % 256 + width)
-            for n in range(tiles):
-                bt = b0 + n
-                rows = slice((bt % 2) * P, (bt % 2 + 1) * P)
+        def score_pass(dst, row_tile, i0, items, half):
+            mx_pass(dst, h_mx[row_tile // 2, half], span(row_tile % 2),
+                    s_mx[i0 // WIDE, half], slice(i0 % WIDE, i0 % WIDE + items), half == 0)
+
+        def scores(i0, items, b0):
+            o_bank[i0, b0] = bank_tile("side", [P, KP // items, items])
+            for n in range(KP // items):
                 for half in range(2):
-                    h_codes, h_scales = h_mx[bt // 2, half]
-                    s_codes, s_scales = s_mx[i0 // 256, half]
-                    nc.tensor.matmul_mx(
-                        out=bank[:, n, :],
-                        lhsT=h_codes[:, rows].bitcast(FP8X4), lhsT_scale=h_scales[:, rows],
-                        rhs=s_codes[:, cols].bitcast(FP8X4), rhs_scale=s_scales[:, cols],
-                        start=(half == 0), stop=(half == 1))
+                    score_pass(o_bank[i0, b0][:, n, :], b0 + n, i0, items, half)
 
-        def store(i0, width, b0, on_scalar):
-            tiles = KP // width
-            res = work.tile([P, tiles, width], F32, name="res", tag="res", bufs=6)
-            if on_scalar:
-                nc.scalar.copy(out=res[:], in_=o_bank[i0, b0][:])
-            else:
-                nc.vector.tensor_copy(out=res[:], in_=o_bank[i0, b0][:])
-            nc.sync.dma_start(out=out[b0 * P:(b0 + tiles) * P, i0:i0 + width].rearrange("(n p) i -> p n i", p=P), in_=res[:])
+        def staging(row_tiles, items):
+            return work.tile([P, row_tiles, items], F32, name="staged", bufs=6)
 
-        def score_pass(dst, bt, i0, width, half):
-            rows = slice((bt % 2) * P, (bt % 2 + 1) * P)
-            cols = slice(i0 % 256, i0 % 256 + width)
-            h_codes, h_scales = h_mx[bt // 2, half]
-            s_codes, s_scales = s_mx[i0 // 256, half]
-            nc.tensor.matmul_mx(
-                out=dst,
-                lhsT=h_codes[:, rows].bitcast(FP8X4), lhsT_scale=h_scales[:, rows],
-                rhs=s_codes[:, cols].bitcast(FP8X4), rhs_scale=s_scales[:, cols],
-                start=(half == 0), stop=(half == 1))
+        def send(staged, i0, b0):
+            row_tiles, items = staged.shape[1], staged.shape[2]
+            nc.sync.dma_start(out=out[b0 * P:(b0 + row_tiles) * P, i0:i0 + items].rearrange("(n p) i -> p n i", p=P),
+                              in_=staged[:])
 
-        widen(0, 0, 0, False)
-        widen(0, 0, 2, True)
-        widen(0, 0, 1, False)
-        widen(0, 0, 3, True)
-        small_step()
-        small_step()
-        widen(1, 0, 0, False)
-        small_step()
+        def store(copy, i0, items, b0):
+            staged = staging(KP // items, items)
+            copy(out=staged[:], in_=o_bank[i0, b0][:])
+            send(staged, i0, b0)
+
+        for t in range(2):
+            widen_on_vector(0, 0, t)
+            widen_on_scalar(0, 0, 2 + t)
+        factor_step()
+        factor_step()
+        widen_on_vector(1, 0, 0)
+        factor_step()
         for t in range(1, T):
-            widen(1, 0, t, True)
+            widen_on_scalar(1, 0, t)
         weave_v(0, 0)
-        small_step()
-        weave_p_pe(0)
-        weave_p_pe(1)
+        factor_step()
+        weave_p_on_tensor(0)
+        weave_p_on_tensor(1)
         nc.scalar.activation(out=g_sign[:], in_=g_sb[:], func=ACT.Sign, bias=floor_col[:], scale=1.0)
         empty_p(0)
-        weave_v(1, 0)
-        small_step()
-        quant_v(0, 0)
-        small_step()
-        quant_p(0)
-        small_step()
-        quant_v(1, 0)
-        small_step()
-        widen(0, 1, 0, True)
+        for job in (lambda: weave_v(1, 0), lambda: quantize_v(0, 0), lambda: quantize_p(0), lambda: quantize_v(1, 0)):
+            job()
+            factor_step()
+        widen_on_scalar(0, 1, 0)
         empty_p(1)
         for t in range(1, T - 1):
-            widen(0, 1, t, True)
-        weave_p_pe(2)
+            widen_on_scalar(0, 1, t)
+        weave_p_on_tensor(2)
         cross(0)
-        quant_p(1)
-        small_step()
+        quantize_p(1)
+        factor_step()
         pieces_bank = turn_pieces()
         empty_p(2)
-        widen(0, 1, T - 1, False)
-        widen(1, 1, 0, False)
+        widen_on_vector(0, 1, T - 1)
+        widen_on_vector(1, 1, 0)
         weave_v(0, 1)
-        weave_p_pe(3)
+        weave_p_on_tensor(3)
 
-        vec_a = {
-            -1: [lambda: quant_p(2), lambda: quant_v(0, 1), lambda: widen(1, 1, 1, False), lambda: widen(1, 1, 2, False)],
-            0: [lambda: quant_p(3), lambda: weave_v(1, 1)],
-            1: [lambda: empty_h(0, 0)],
-            2: [lambda: empty_h(0, 1)],
-            3: [lambda: empty_h(1, 0)],
-            4: [lambda: weave_p(4)],
-            5: [lambda: empty_h(1, 1)],
-            6: [lambda: weave_p(5)],
-            7: [lambda: empty_h(2, 0)],
-            8: [lambda: weave_p(6), lambda: empty_h(2, 1)],
-            9: [lambda: empty_h(3, 0), lambda: quant_h(2, 1)],
-            10: [lambda: empty_h(3, 1), lambda: weave_p(7)],
-            11: [lambda: store(256, 256, 2, False), lambda: store(256, 256, 4, False)],
-            12: [lambda: store(512, 128, 0, False)],
-            13: [lambda: store(256, 256, 6, False), lambda: store(512, 128, 4, False)],
-            14: [lambda: store(640, 128, 0, False)],
-        }
-        vec_b = {
-            -1: [lambda: widen(1, 1, 3, False)],
-            0: [lambda: quant_v(1, 1)],
-            1: [lambda: quant_h(0, 0)],
-            2: [lambda: quant_h(0, 1)],
-            3: [lambda: quant_h(1, 0)],
-            4: [lambda: quant_p(4)],
-            5: [lambda: quant_h(1, 1)],
-            6: [lambda: quant_p(5)],
-            7: [lambda: quant_h(2, 0)],
-            8: [lambda: quant_p(6)],
-            9: [lambda: quant_h(3, 0)],
-            10: [lambda: quant_h(3, 1), lambda: quant_p(7)],
-            14: [lambda: store(640, 128, 4, False), lambda: scores(768, 128, 0), lambda: scores(768, 128, 4)],
-        }
-        act = {
-            -1: [lambda: nc.scalar.copy(out=d_lhs[:], in_=pieces_bank[:])],
-            0: [lambda: empty_p(3)],
-            8: [lambda: store(0, 256, 0, True)],
-            9: [lambda: store(0, 256, 2, True)],
-            10: [lambda: store(256, 256, 0, True)],
-            11: [lambda: store(0, 256, 4, True)],
-            13: [lambda: store(0, 256, 6, True)],
-        }
-        pe = {
-            0: [lambda: turn_h(0, 0)],
-            1: [lambda: turn_h(0, 1)],
-            2: [lambda: turn_h(1, 0)],
-            4: [lambda: turn_h(1, 1)],
-            6: [lambda: turn_h(2, 0)],
-            7: [lambda: scores(0, 256, 0), lambda: turn_h(2, 1)],
-            8: [lambda: scores(0, 256, 2), lambda: turn_h(3, 0)],
-            9: [lambda: scores(256, 256, 0), lambda: turn_h(3, 1)],
-            10: [lambda: scores(0, 256, 4), lambda: scores(256, 256, 2), lambda: scores(256, 256, 4)],
-            11: [lambda: scores(512, 128, 0)],
-            12: [lambda: scores(0, 256, 6), lambda: scores(256, 256, 6), lambda: scores(512, 128, 4)],
-            13: [lambda: scores(640, 128, 0)],
-            14: [lambda: scores(640, 128, 4)],
-        }
-        last = len(BANKS) - 1
+        p_step, h_step = plan_operands()
+        multiplied = plan_outputs(h_step)
+        on_scalar, before, after, on_tensor = [{k: [] for k in range(-1, LAST)} for n in range(4)]
+        on_scalar[-1].append(lambda: nc.scalar.copy(out=d_stationary[:], in_=pieces_bank[:]))
+        on_scalar[0].append(lambda: empty_p(3))
+        before[-1].extend([lambda: quantize_p(2), lambda: quantize_v(0, 1),
+                           lambda: widen_on_vector(1, 1, 1), lambda: widen_on_vector(1, 1, 2)])
+        after[-1].append(lambda: widen_on_vector(1, 1, 3))
+        before[0].extend([lambda: quantize_p(3), lambda: weave_v(1, 1)])
+        after[0].append(lambda: quantize_v(1, 1))
+        for k, banks in multiplied.items():
+            for n, bank in enumerate(banks):
+                on_tensor[k].append(lambda bank=bank: scores(*bank))
+                if n == 0 and k + 1 <= LAST_SCALAR_COPY_STEP:
+                    on_scalar[k + 1].append(lambda bank=bank: store(nc.scalar.copy, *bank))
+                else:
+                    jobs = before[k + 1] if k + 1 < LAST else after[k]
+                    jobs.append(lambda bank=bank: store(nc.vector.tensor_copy, *bank))
+        for chunk, k in p_step.items():
+            before[k].append(lambda chunk=chunk: weave_p_on_vector(chunk))
+            after[k].append(lambda chunk=chunk: quantize_p(chunk))
+        for key, k in h_step.items():
+            on_tensor[k - 1].append(lambda key=key: turn_h(*key))
+            before[k].append(lambda key=key: empty_h(*key))
+            after[k].append(lambda key=key: quantize_h(*key))
 
-        def run(jobs, k):
-            for job in jobs.get(k, []):
+        def run(jobs):
+            for job in jobs:
                 job()
 
-        for k in range(-1, last):
-            do_w(k + 1)
-            run(act, k)
-            if k + 2 <= last:
+        for k in range(-1, LAST):
+            take_root(k + 1)
+            run(on_scalar[k])
+            if k + 2 <= LAST:
                 cross(k + 2)
-            run(vec_a, k)
+            run(before[k])
             norms(k + 1)
-            run(pe, k)
-            if 0 <= k - 1:
-                do_y2(k - 1)
-                do_s(k - 1)
-            if k + 1 <= last:
-                do_z(k + 1)
-                do_den(k + 1)
-            if 0 <= k <= last:
-                do_y(k)
-            if 0 <= k - 1:
-                quant_s(k - 1)
-            run(vec_b, k)
-        halves = [slice(0, P // 2), slice(P // 2, P)]
-        do_y2(last - 1)
-        do_s(last - 1)
+            run(on_tensor[k])
+            if k >= 1:
+                take_recip(k - 1)
+                take_s(k - 1)
+            take_ratio(k + 1)
+            take_den(k + 1)
+            if k >= 0:
+                take_den_root(k)
+            if k >= 1:
+                quantize_s(k - 1)
+            run(after[k])
+
+        next_to_last = [((CHUNKS - 2) * P, P, b0) for b0 in range(0, B // P, T)]
+        for bank in next_to_last:
+            scores(*bank)
+        halves = [span(n, P // 4) for n in range(2)]
+        take_recip(LAST - 1)
+        take_s(LAST - 1)
         for part in halves:
-            do_y(last, part)
+            take_den_root(LAST, part)
         for part in halves:
-            do_y2(last, part)
-        quant_s(last - 1)
+            take_recip(LAST, part)
+        quantize_s(LAST - 1)
         for part in halves:
-            do_s(last, part)
-        store(768, 128, 0, True)
-        store(768, 128, 4, True)
-        tags = [("c_bank", 4), ("c_bank", 4), ("d_bank", 1), ("side", 3), ("c_bank", 4), ("side", 3), ("c_bank", 4)]
+            take_s(LAST, part)
+        for bank in next_to_last:
+            store(nc.scalar.copy, *bank)
+        i0 = (CHUNKS - 1) * P
         tail = []
-        for bt, (tag, bufs) in enumerate(tags):
-            bank = psum.tile([P, P], F32, name=tag, tag=tag, bufs=bufs)
-            tail.append(bank)
-            score_pass(bank[:], bt, 896, P, 0)
-        quant_s(last)
-        for bt in range(7):
-            score_pass(tail[bt][:], bt, 896, P, 1)
-        bank = side_bank([P, P], F32)
-        tail.append(bank)
+        for row_tile, tag in enumerate(["c", "c", "d", "side", "c", "side", "c"]):
+            tail.append(bank_tile(tag, [P, P]))
+            score_pass(tail[row_tile][:], row_tile, i0, P, 0)
+        quantize_s(LAST)
+        for row_tile in range(len(tail)):
+            score_pass(tail[row_tile][:], row_tile, i0, P, 1)
+        tail.append(bank_tile("side", [P, P]))
         for half in range(2):
-            score_pass(bank[:], 7, 896, P, half)
-        for pair in range(4):
-            res = work.tile([P, 2, P], F32, name="res", tag="res", bufs=6)
-            nc.scalar.copy(out=res[:, 0, :], in_=tail[2 * pair][:])
-            nc.vector.tensor_copy(out=res[:, 1, :], in_=tail[2 * pair + 1][:])
-            nc.sync.dma_start(out=out[2 * pair * P:(2 * pair + 2) * P, 896:1024].rearrange("(n p) i -> p n i", p=P), in_=res[:])
+            score_pass(tail[-1][:], len(tail) - 1, i0, P, half)
+        for b0 in range(0, B // P, 2):
+            staged = staging(2, P)
+            nc.scalar.copy(out=staged[:, 0, :], in_=tail[b0][:])
+            nc.vector.tensor_copy(out=staged[:, 1, :], in_=tail[b0 + 1][:])
+            send(staged, i0, b0)

@@ -36,14 +36,12 @@ BANKS = ([(chunk, half) for half in range(2) for chunk in range(EARLY)]
          + [(chunk, half) for chunk in range(EARLY, CHUNKS) for half in range(2)])
 LAST = len(BANKS) - 1
 
-FIRST_COPY_STEP = 8
-LAST_SCALAR_COPY_STEP = 11
+LAST_SCALAR_COPY_STEP = 9
 
 
 def plan_operands():
-    p_step = {chunk: BANKS.index((chunk, 0)) - 4 for chunk in range(EARLY, CHUNKS)}
-    free = [k for k in range(1, LAST) if k >= FIRST_COPY_STEP or k not in p_step.values()]
-    h_step = dict(zip([(pair, half) for pair in range(B // WIDE) for half in range(2)], free))
+    h_step = {(pair, half): 1 + 2 * pair + half for pair in range(B // WIDE) for half in range(2)}
+    p_step = {chunk: 2 * (chunk - EARLY) + 3 for chunk in range(EARLY, CHUNKS)}
     return p_step, h_step
 
 
@@ -60,7 +58,7 @@ def plan_outputs(h_step):
     waiting = sorted(banks, key=ready)
     by_step = {}
     for k in range(LAST):
-        room = 1 if k < max(h_step.values()) else 2
+        room = 2 if k >= max(h_step.values()) and len(waiting) > LAST - k else 1
         by_step[k] = [bank for bank in waiting[:room] if ready(bank) <= k]
         waiting = waiting[len(by_step[k]):]
     assert not waiting
@@ -69,6 +67,7 @@ def plan_outputs(h_step):
 
 def tile_crossoccurrencedampedscores_kernel(tc, p, v_bytes, v_scale, n_p, n_v, g, h, out):
     nc = tc.nc
+    p_step, h_step = plan_operands()
     with ExitStack() as ctx:
         keep = ctx.enter_context(tc.tile_pool(name="keep", bufs=1))
         work = ctx.enter_context(tc.tile_pool(name="work", bufs=2))
@@ -146,8 +145,8 @@ def tile_crossoccurrencedampedscores_kernel(tc, p, v_bytes, v_scale, n_p, n_v, g
         pieces = kept([P, 2 * T, P], BF16, "pieces")
         nc.vector.memset(pieces[:], 0.0)
         nc.scalar.activation(out=table_warm[:], in_=floor_col[:], func=ACT.Abs_reciprocal_sqrt, bias=floor_col[:], scale=1.0)
-        make_identity(nc, ident_bf[:])
         make_identity(nc, ident_f32[:])
+        nc.scalar.copy(out=ident_bf[:], in_=ident_f32[:])
 
         g_abs = kept([P, 2 * T], F32, "g_abs")
         g_bounded = kept([P, 2 * T], F32, "g_bounded")
@@ -210,9 +209,8 @@ def tile_crossoccurrencedampedscores_kernel(tc, p, v_bytes, v_scale, n_p, n_v, g
         def p_chunk(chunk):
             return p_raw[chunk // 2][:, :, :, span(chunk % 2)]
 
-        def new_p_woven(chunk):
-            p_woven[chunk] = work.tile([P, 2 * KP], BF16, name="p_woven", bufs=3, align_bytes=64)
-            return p_woven[chunk]
+        def woven_tile(step):
+            return work.tile([P, 2 * KP], BF16, name="woven_%d" % (step % 2), bufs=1, align_bytes=64)
 
         def weave_p_on_tensor(chunk):
             p_bank[chunk] = bank_tile("side", [P, 2, P, T], BF16)
@@ -221,11 +219,14 @@ def tile_crossoccurrencedampedscores_kernel(tc, p, v_bytes, v_scale, n_p, n_v, g
                                  rhs=p_chunk(chunk)[:, a, :, :].rearrange("p t i -> p i t"), start=True, stop=True)
 
         def empty_p(chunk):
-            nc.scalar.copy(out=new_p_woven(chunk)[:], in_=p_bank[chunk][:].rearrange("p a i t -> p (a i t)"))
+            p_woven[chunk] = work.tile([P, 2 * KP], BF16, name="p_woven", bufs=3, align_bytes=64)
+            nc.scalar.copy(out=p_woven[chunk][:], in_=p_bank[chunk][:].rearrange("p a i t -> p (a i t)"))
 
-        def weave_p_on_vector(chunk):
-            nc.vector.tensor_copy(out=new_p_woven(chunk)[:].rearrange("p (a c e t) -> p a c t e", a=2, t=T, e=4),
-                                  in_=p_chunk(chunk).rearrange("p a t (c e) -> p a c t e", e=4))
+        def weave_p_on_gpsimd(chunk):
+            p_woven[chunk] = woven_tile(p_step[chunk] - 1)
+            nc.gpsimd.tensor_scalar(out=p_woven[chunk][:].rearrange("p (a i t) -> p a i t", a=2, t=T),
+                                    in0=p_chunk(chunk).rearrange("p a t i -> p a i t"),
+                                    scalar1=1.0, scalar2=0.0, op0=ALU.mult, op1=ALU.add)
 
         def quantize_p(chunk):
             p_mx[chunk] = mx_tiles(WIDE, "p_%d" % chunk)
@@ -242,7 +243,7 @@ def tile_crossoccurrencedampedscores_kernel(tc, p, v_bytes, v_scale, n_p, n_v, g
                                         words[:, WIDE * half + u:WIDE * (half + 1):2], ident_f32[:])
 
         def empty_h(pair, half):
-            h_woven[pair, half] = work.tile([P, WIDE * T], BF16, name="h_woven", bufs=3, align_bytes=64)
+            h_woven[pair, half] = woven_tile(h_step[pair, half])
             turned = h_bank[pair, half][:].rearrange("p u r b -> p (u r b)").bitcast(BF16)
             signs = g_sign[:, half, :].rearrange("p (u e) -> p u e", u=2).unsqueeze(1)
             nc.vector.tensor_tensor(
@@ -372,7 +373,6 @@ def tile_crossoccurrencedampedscores_kernel(tc, p, v_bytes, v_scale, n_p, n_v, g
         weave_v(0, 1)
         weave_p_on_tensor(3)
 
-        p_step, h_step = plan_operands()
         multiplied = plan_outputs(h_step)
         on_scalar, before, after, on_tensor = [{k: [] for k in range(-1, LAST)} for n in range(4)]
         on_scalar[-1].append(lambda: nc.scalar.copy(out=d_stationary[:], in_=pieces_bank[:]))
@@ -391,7 +391,7 @@ def tile_crossoccurrencedampedscores_kernel(tc, p, v_bytes, v_scale, n_p, n_v, g
                     jobs = before[k + 1] if k + 1 < LAST else after[k]
                     jobs.append(lambda bank=bank: store(nc.vector.tensor_copy, *bank))
         for chunk, k in p_step.items():
-            before[k].append(lambda chunk=chunk: weave_p_on_vector(chunk))
+            before[k].append(lambda chunk=chunk: weave_p_on_gpsimd(chunk))
             after[k].append(lambda chunk=chunk: quantize_p(chunk))
         for key, k in h_step.items():
             on_tensor[k - 1].append(lambda key=key: turn_h(*key))

from contextlib import ExitStack

import concourse.mybir as mybir
from concourse.masks import make_identity

U = I = J = B = 1024
FLOPS = 2 * U * I * J + 2 * B * I * J

F32 = mybir.dt.float32
BF16 = mybir.dt.bfloat16
U32 = mybir.dt.uint32
U8 = mybir.dt.uint8
FP8 = mybir.dt.float8_e4m3fn
FP8X4 = mybir.dt.float8_e4m3fn_x4
ACT = mybir.ActivationFunctionType
ALU = mybir.AluOpType

P = 128
T = 4
KP = P * T
WIDE = 2 * P
CHUNKS = I // P
ROOT_U = 32.0
SHRINK_SIM = 0.5
SHRINK_DAMP = 0.5
DAMP = ROOT_U * SHRINK_DAMP
C_FLOOR = 2.0 ** -60
G_FLOOR = 2.0 ** -50
PIECES = 3
ONES_ROW = 32

C_BANKS, D_BANKS, SIDE_BANKS = 4, 1, 3

EARLY = 4
BANKS = ([(chunk, half) for half in range(2) for chunk in range(EARLY)]
         + [(chunk, half) for chunk in range(EARLY, CHUNKS) for half in range(2)])
LAST = len(BANKS) - 1

LAST_SCALAR_COPY_STEP = 9


def plan_operands():
    h_step = {(pair, half): 1 + 2 * pair + half for pair in range(B // WIDE) for half in range(2)}
    p_step = {chunk: 2 * (chunk - EARLY) + 3 for chunk in range(EARLY, CHUNKS)}
    return p_step, h_step


def plan_outputs(h_step):
    banks = [(i0, WIDE, b0) for i0 in range(0, EARLY * P, WIDE) for b0 in range(0, B // P, 2)]
    banks = banks + [(chunk * P, P, b0) for chunk in range(EARLY, CHUNKS - 2) for b0 in range(0, B // P, T)]

    def ready(bank):
        i0, items, b0 = bank
        s_done = BANKS.index(((i0 + items) // P - 1, 1)) + 1
        h_done = h_step[(b0 + KP // items - 1) // 2, 1]
        return max(s_done, h_done) + 1

    waiting = sorted(banks, key=ready)
    by_step = {}
    for k in range(LAST):
        room = 2 if k >= max(h_step.values()) and len(waiting) > LAST - k else 1
        by_step[k] = [bank for bank in waiting[:room] if ready(bank) <= k]
        waiting = waiting[len(by_step[k]):]
    assert not waiting
    return by_step


def tile_crossoccurrencedampedscores_kernel(tc, p, v_bytes, v_scale, n_p, n_v, g, h, out):
    nc = tc.nc
    p_step, h_step = plan_operands()
    with ExitStack() as ctx:
        keep = ctx.enter_context(tc.tile_pool(name="keep", bufs=1))
        work = ctx.enter_context(tc.tile_pool(name="work", bufs=2))
        psum = ctx.enter_context(tc.psum_pool(name="psum", bufs=1))
        ctx.enter_context(tc.manual_schedule())

        def kept(shape, dtype, name):
            return keep.tile(shape, dtype, name=name, align_bytes=64)

        def mx_tiles(words, name):
            return kept([P, words], U32, name + "_codes"), kept([P, words], U8, name + "_scales")

        def bank_tile(tag, shape, dtype=F32):
            bufs = {"c": C_BANKS, "d": D_BANKS, "side": SIDE_BANKS}[tag]
            return psum.tile(shape, dtype, name=tag + "_bank", tag=tag, bufs=bufs)

        def quantize(woven, codes, scales):
            nc.vector.quantize_mx(out=codes.bitcast(FP8X4), scales=scales, in_=woven)

        def mx_pass(dst, stationary, m_cols, moving, n_cols, first):
            nc.tensor.matmul_mx(
                out=dst,
                lhsT=stationary[0][:, m_cols].bitcast(FP8X4), lhsT_scale=stationary[1][:, m_cols],
                rhs=moving[0][:, n_cols].bitcast(FP8X4), rhs_scale=moving[1][:, n_cols],
                start=first, stop=not first)

        def span(n, width=P):
            return slice(n * width, (n + 1) * width)

        vs = kept([P, 2, T], F32, "vs")
        g_sb = kept([P, 2, T], BF16, "g_sb")
        nv_sb = kept([P, 2, T], BF16, "nv_sb")
        d_moving = kept([P, I], BF16, "d_moving")
        floor_col = kept([P, 1], F32, "floor_col")
        nc.vector.memset(floor_col[:], C_FLOOR)
        nc.vector.memset(d_moving[:], 1.0)
        nc.scalar.dma_start(out=vs[:], in_=v_scale.rearrange("(a p t) o -> p a (t o)", p=P, t=T))

        v_rows = v_bytes.rearrange("(a p t) j -> a p t j", p=P, t=T)
        p_rows = p.rearrange("(a p t) i -> a p t i", p=P, t=T)
        h_rows = h.rearrange("(q r p) j -> q p r j", p=P, r=2)
        v_raw, p_raw, h_raw = {}, {}, {}

        def load_v(a, half):
            v_raw[a, half] = kept([P, T, KP], U8, "v_raw_%d_%d" % (a, half))
            nc.sync.dma_start(out=v_raw[a, half][:], in_=v_rows[a][:, :, span(half, KP)])

        def load_p(quarter):
            p_raw[quarter] = kept([P, 2, T, WIDE], BF16, "p_raw_%d" % quarter)
            for a in range(2):
                nc.sync.dma_start(out=p_raw[quarter][:, a, :, :], in_=p_rows[a][:, :, span(quarter, WIDE)])

        def load_h(pair):
            h_raw[pair] = kept([P, 2, J], BF16, "h_raw_%d" % pair)
            nc.sync.dma_start(out=h_raw[pair][:], in_=h_rows[pair])

        load_v(0, 0)
        nc.sync.dma_start(out=g_sb[:], in_=g.rearrange("(a p t) -> p a t", p=P, t=T))
        nc.sync.dma_start(out=nv_sb[:], in_=n_v.rearrange("(a p t) -> p a t", p=P, t=T))
        load_v(1, 0)
        load_p(0)
        nc.sync.dma_start(out=d_moving[0:4, :], in_=n_p.partition_broadcast(4))
        load_v(0, 1)
        load_p(1)
        load_v(1, 1)
        for n in range(2):
            load_h(n)
            load_p(2 + n)
        load_h(2)
        load_h(3)

        ident_bf = kept([P, P], BF16, "ident_bf")
        ident_f32 = kept([P, P], F32, "ident_f32")
        table_warm = kept([P, 1], F32, "table_warm")
        pieces = kept([P, 2 * T, P], BF16, "pieces")
        nc.vector.memset(pieces[:], 0.0)
        nc.scalar.activation(out=table_warm[:], in_=floor_col[:], func=ACT.Abs_reciprocal_sqrt, bias=floor_col[:], scale=1.0)
        make_identity(nc, ident_f32[:])
        nc.scalar.copy(out=ident_bf[:], in_=ident_f32[:])

        g_abs = kept([P, 2 * T], F32, "g_abs")
        g_bounded = kept([P, 2 * T], F32, "g_bounded")
        rest = [kept([P, 2, 2 * T], F32, "rest_%d" % n) for n in range(PIECES)]
        g_sign = kept([P, 2, T], BF16, "g_sign")
        d_stationary = kept([P, 2 * T, P], BF16, "d_stationary")
        g_flat = g_sb[:].rearrange("p a t -> p (a t)")
        nv_flat = nv_sb[:].rearrange("p a t -> p (a t)")

        def piece(n):
            return pieces[:].rearrange("p s (f x) -> p f s x", x=ONES_ROW)[:, 0:2, :, n]

        factor_steps = [
            lambda: nc.vector.scalar_tensor_tensor(out=g_abs[:], in0=g_flat, scalar=-1.0, in1=g_flat,
                                                   op0=ALU.mult, op1=ALU.max),
            lambda: nc.vector.tensor_scalar(out=g_bounded[:], in0=g_abs[:], scalar1=G_FLOOR,
                                            scalar2=1.0 / (ROOT_U * SHRINK_SIM), op0=ALU.max, op1=ALU.mult),
            lambda: nc.vector.reciprocal(out=rest[0][:, 1, :], in_=g_bounded[:]),
            lambda: nc.vector.scalar_tensor_tensor(out=rest[0][:, 0, :], in0=nv_flat, scalar=1.0 / SHRINK_SIM,
                                                   in1=rest[0][:, 1, :], op0=ALU.mult, op1=ALU.mult),
        ]
        for n in range(PIECES):
            factor_steps.append(lambda n=n: nc.vector.tensor_copy(out=piece(n), in_=rest[n][:]))
            if n + 1 < PIECES:
                factor_steps.append(lambda n=n: nc.vector.tensor_tensor(out=rest[n + 1][:], in0=rest[n][:],
                                                                        in1=piece(n), op=ALU.subtract))

        def factor_step():
            factor_steps.pop(0)()

        def turn_pieces():
            bank = bank_tile("side", [P, 2 * T, P], BF16)
            for s in range(2 * T):
                nc.tensor.transpose(bank[:, s, :], pieces[:, s, :], ident_bf[:])
            return bank

        v_wide = {key: kept([P, T, KP], BF16, "v_wide_%d_%d" % key) for key in v_raw}
        v_woven, v_mx = {}, {}

        def widen_on_scalar(a, half, t):
            nc.scalar.activation(out=v_wide[a, half][:, t, :], in_=v_raw[a, half][:, t, :].bitcast(FP8),
                                 func=ACT.Copy, scale=vs[:, a, t:t + 1])

        def widen_on_vector(a, half, t):
            nc.vector.tensor_scalar(out=v_wide[a, half][:, t, :], in0=v_raw[a, half][:, t, :].bitcast(FP8),
                                    scalar1=vs[:, a, t:t + 1], scalar2=None, op0=ALU.mult)

        def weave_v(a, half):
            v_woven[a, half] = work.tile([P, T * KP], BF16, name="v_woven", align_bytes=64)
            nc.vector.tensor_copy(
                out=v_woven[a, half][:].rearrange("p (s m e t) -> p m s t e", s=T, t=T, e=2),
                in_=v_wide[a, half][:].rearrange("p t (m e s) -> p m s t e", s=T, e=2))

        def quantize_v(a, half):
            v_mx[a, half] = mx_tiles(KP, "v_%d_%d" % (a, half))
            quantize(v_woven[a, half][:], v_mx[a, half][0][:], v_mx[a, half][1][:])

        p_bank, p_woven, p_mx = {}, {}, {}

        def p_chunk(chunk):
            return p_raw[chunk // 2][:, :, :, span(chunk % 2)]

        def woven_tile(step):
            return work.tile([P, 2 * KP], BF16, name="woven_%d" % (step % 2), bufs=1, align_bytes=64)

        def weave_p_on_tensor(chunk):
            p_bank[chunk] = bank_tile("side", [P, 2, P, T], BF16)
            for a in range(2):
                nc.tensor.matmul(p_bank[chunk][:, a, :, :], lhsT=ident_bf[:],
                                 rhs=p_chunk(chunk)[:, a, :, :].rearrange("p t i -> p i t"), start=True, stop=True)

        def empty_p(chunk):
            p_woven[chunk] = work.tile([P, 2 * KP], BF16, name="p_woven", bufs=3, align_bytes=64)
            nc.scalar.copy(out=p_woven[chunk][:], in_=p_bank[chunk][:].rearrange("p a i t -> p (a i t)"))

        def weave_p_on_gpsimd(chunk):
            p_woven[chunk] = woven_tile(p_step[chunk] - 1)
            nc.gpsimd.tensor_scalar(out=p_woven[chunk][:].rearrange("p (a i t) -> p a i t", a=2, t=T),
                                    in0=p_chunk(chunk).rearrange("p a t i -> p a i t"),
                                    scalar1=1.0, scalar2=0.0, op0=ALU.mult, op1=ALU.add)

        def quantize_p(chunk):
            p_mx[chunk] = mx_tiles(WIDE, "p_%d" % chunk)
            quantize(p_woven[chunk][:], p_mx[chunk][0][:], p_mx[chunk][1][:])

        h_bank, h_woven, h_mx = {}, {}, {}

        def turn_h(pair, half):
            h_bank[pair, half] = bank_tile("side", [P, 2, 2, P])
            for r in range(2):
                words = h_raw[pair][:, r, :].bitcast(F32)
                for u in range(2):
                    nc.tensor.transpose(h_bank[pair, half][:, u, r, :],
                                        words[:, WIDE * half + u:WIDE * (half + 1):2], ident_f32[:])

        def empty_h(pair, half):
            h_woven[pair, half] = woven_tile(h_step[pair, half])
            turned = h_bank[pair, half][:].rearrange("p u r b -> p (u r b)").bitcast(BF16)
            signs = g_sign[:, half, :].rearrange("p (u e) -> p u e", u=2).unsqueeze(1)
            nc.vector.tensor_tensor(
                out=h_woven[pair, half][:].rearrange("p (b u e) -> p b u e", u=2, e=2),
                in0=turned.rearrange("p (u b e) -> p b u e", u=2, e=2),
                in1=signs.to_broadcast([P, WIDE, 2, 2]), op=ALU.mult)

        def quantize_h(pair, half):
            h_mx[pair, half] = mx_tiles(WIDE, "h_%d_%d" % (pair, half))
            quantize(h_woven[pair, half][:], h_mx[pair, half][0][:], h_mx[pair, half][1][:])

        c_bank, d_bank, root, ratio, den, den_root, recip, s_woven, s_mx = {}, {}, {}, {}, {}, {}, {}, {}, {}
        whole = slice(0, P // 2)

        def chain_tile(tiles, k, name):
            if k not in tiles:
                tiles[k] = work.tile([P, P // 2, T * 2], F32, name=name)
            return tiles[k]

        def c_pairs(k):
            return c_bank[k][:].rearrange("p t (c e) -> p c t e", e=2)

        def cross(k):
            chunk, half = BANKS[k]
            c_bank[k] = bank_tile("c", [P, T, P])
            for t in range(T):
                for a in range(2):
                    mx_pass(c_bank[k][:, t, :], v_mx[a, half], span(t), p_mx[chunk], span(a), a == 0)

        def norms(k):
            chunk, half = BANKS[k]
            d_bank[k] = bank_tile("d", [P, P // 2, T, 2])
            for t in range(T):
                nc.tensor.matmul(d_bank[k][:, :, t, :], lhsT=d_stationary[:, half * T + t, :],
                                 rhs=d_moving[:, span(chunk)].rearrange("p (c e) -> p c e", e=2),
                                 start=True, stop=True)

        def take_root(k):
            nc.scalar.activation(out=chain_tile(root, k, "root")[:].rearrange("p c (t e) -> p c t e", e=2),
                                 in_=c_pairs(k), func=ACT.Abs_reciprocal_sqrt, bias=floor_col[:], scale=1.0 / DAMP)

        def take_ratio(k):
            nc.scalar.activation(out=chain_tile(ratio, k, "ratio")[:], in_=root[k][:], func=ACT.Square)

        def take_den(k):
            nc.vector.scalar_tensor_tensor(out=chain_tile(den, k, "den")[:], in0=ratio[k][:], scalar=1.0,
                                           in1=d_bank[k][:].rearrange("p c t e -> p c (t e)"),
                                           op0=ALU.add, op1=ALU.mult)

        def take_den_root(k, part=whole):
            nc.scalar.activation(out=chain_tile(den_root, k, "den_root")[:, part, :], in_=den[k][:, part, :],
                                 func=ACT.Abs_reciprocal_sqrt)

        def take_recip(k, part=whole):
            nc.scalar.activation(out=chain_tile(recip, k, "recip")[:, part, :], in_=den_root[k][:, part, :],
                                 func=ACT.Square)

        def take_s(k, part=whole):
            if k not in s_woven:
                s_woven[k] = work.tile([P, P, T], BF16, name="s_woven", align_bytes=64)
            nc.vector.tensor_tensor(
                out=s_woven[k][:].rearrange("p (c e) t -> p c t e", e=2)[:, part, :, :], in0=c_pairs(k)[:, part, :, :],
                in1=recip[k][:, part, :].rearrange("p c (t e) -> p c t e", e=2), op=ALU.mult)

        def quantize_s(k):
            chunk, half = BANKS[k]
            if (chunk // 2, half) not in s_mx:
                s_mx[chunk // 2, half] = mx_tiles(WIDE, "s_%d_%d" % (chunk // 2, half))
            codes, scales = s_mx[chunk // 2, half]
            quantize(s_woven[k][:].rearrange("p i t -> p (i t)"), codes[:, span(chunk % 2)], scales[:, span(chunk % 2)])

        o_bank = {}

        def score_pass(dst, row_tile, i0, items, half):
            mx_pass(dst, h_mx[row_tile // 2, half], span(row_tile % 2),
                    s_mx[i0 // WIDE, half], slice(i0 % WIDE, i0 % WIDE + items), half == 0)

        def scores(i0, items, b0):
            o_bank[i0, b0] = bank_tile("side", [P, KP // items, items])
            for n in range(KP // items):
                for half in range(2):
                    score_pass(o_bank[i0, b0][:, n, :], b0 + n, i0, items, half)

        def staging(row_tiles, items):
            return work.tile([P, row_tiles, items], F32, name="staged", bufs=6)

        def send(staged, i0, b0):
            row_tiles, items = staged.shape[1], staged.shape[2]
            nc.sync.dma_start(out=out[b0 * P:(b0 + row_tiles) * P, i0:i0 + items].rearrange("(n p) i -> p n i", p=P),
                              in_=staged[:])

        def store(copy, i0, items, b0):
            staged = staging(KP // items, items)
            copy(out=staged[:], in_=o_bank[i0, b0][:])
            send(staged, i0, b0)

        for t in range(2):
            widen_on_vector(0, 0, t)
            widen_on_scalar(0, 0, 2 + t)
        factor_step()
        factor_step()
        widen_on_vector(1, 0, 0)
        factor_step()
        for t in range(1, T):
            widen_on_scalar(1, 0, t)
        weave_v(0, 0)
        factor_step()
        weave_p_on_tensor(0)
        weave_p_on_tensor(1)
        nc.scalar.activation(out=g_sign[:], in_=g_sb[:], func=ACT.Sign, bias=floor_col[:], scale=1.0)
        empty_p(0)
        for job in (lambda: weave_v(1, 0), lambda: quantize_v(0, 0), lambda: quantize_p(0), lambda: quantize_v(1, 0)):
            job()
            factor_step()
        widen_on_scalar(0, 1, 0)
        empty_p(1)
        for t in range(1, T - 1):
            widen_on_scalar(0, 1, t)
        weave_p_on_tensor(2)
        cross(0)
        quantize_p(1)
        factor_step()
        pieces_bank = turn_pieces()
        empty_p(2)
        widen_on_vector(0, 1, T - 1)
        widen_on_vector(1, 1, 0)
        weave_v(0, 1)
        weave_p_on_tensor(3)

        multiplied = plan_outputs(h_step)
        on_scalar, before, after, on_tensor = [{k: [] for k in range(-1, LAST)} for n in range(4)]
        on_scalar[-1].append(lambda: nc.scalar.copy(out=d_stationary[:], in_=pieces_bank[:]))
        on_scalar[0].append(lambda: empty_p(3))
        before[-1].extend([lambda: quantize_p(2), lambda: quantize_v(0, 1),
                           lambda: widen_on_vector(1, 1, 1), lambda: widen_on_vector(1, 1, 2)])
        after[-1].append(lambda: widen_on_vector(1, 1, 3))
        before[0].extend([lambda: quantize_p(3), lambda: weave_v(1, 1)])
        after[0].append(lambda: quantize_v(1, 1))
        for k, banks in multiplied.items():
            for n, bank in enumerate(banks):
                on_tensor[k].append(lambda bank=bank: scores(*bank))
                if n == 0 and k + 1 <= LAST_SCALAR_COPY_STEP:
                    on_scalar[k + 1].append(lambda bank=bank: store(nc.scalar.copy, *bank))
                else:
                    jobs = before[k + 1] if k + 1 < LAST else after[k]
                    jobs.append(lambda bank=bank: store(nc.vector.tensor_copy, *bank))
        for chunk, k in p_step.items():
            before[k].append(lambda chunk=chunk: weave_p_on_gpsimd(chunk))
            after[k].append(lambda chunk=chunk: quantize_p(chunk))
        for key, k in h_step.items():
            on_tensor[k - 1].append(lambda key=key: turn_h(*key))
            before[k].append(lambda key=key: empty_h(*key))
            after[k].append(lambda key=key: quantize_h(*key))

        def run(jobs):
            for job in jobs:
                job()

        for k in range(-1, LAST):
            take_root(k + 1)
            run(on_scalar[k])
            if k + 2 <= LAST:
                cross(k + 2)
            run(before[k])
            norms(k + 1)
            run(on_tensor[k])
            if k >= 1:
                take_recip(k - 1)
                take_s(k - 1)
            take_ratio(k + 1)
            take_den(k + 1)
            if k >= 0:
                take_den_root(k)
            if k >= 1:
                quantize_s(k - 1)
            run(after[k])

        next_to_last = [((CHUNKS - 2) * P, P, b0) for b0 in range(0, B // P, T)]
        for bank in next_to_last:
            scores(*bank)
        halves = [span(n, P // 4) for n in range(2)]
        take_recip(LAST - 1)
        take_s(LAST - 1)
        for part in halves:
            take_den_root(LAST, part)
        for part in halves:
            take_recip(LAST, part)
        quantize_s(LAST - 1)
        for part in halves:
            take_s(LAST, part)
        for bank in next_to_last:
            store(nc.scalar.copy, *bank)
        i0 = (CHUNKS - 1) * P
        tail = []
        for row_tile, tag in enumerate(["c", "c", "d", "side", "c", "side", "c"]):
            tail.append(bank_tile(tag, [P, P]))
            score_pass(tail[row_tile][:], row_tile, i0, P, 0)
        quantize_s(LAST)
        for row_tile in range(len(tail)):
            score_pass(tail[row_tile][:], row_tile, i0, P, 1)
        tail.append(bank_tile("side", [P, P]))
        for half in range(2):
            score_pass(tail[-1][:], len(tail) - 1, i0, P, half)
        for b0 in range(0, B // P, 2):
            staged = staging(2, P)
            nc.scalar.copy(out=staged[:, 0, :], in_=tail[b0][:])
            nc.vector.tensor_copy(out=staged[:, 1, :], in_=tail[b0 + 1][:])
            send(staged, i0, b0)
